import numpy as np
CORES = [36,164,52,180,100,228,116,244]
N = 8
T, FF, CAP, CAPP = 4096, 2, 1024, 256
def entries(a): return a.T.reshape(-1)
def pack(v, P): return np.ascontiguousarray(np.asarray(v, np.int32).reshape(-1, P).T)
def lists(rng, how):
    O = np.stack([rng.permutation(np.repeat(np.arange(N), CAPP))[:CAP] for k in range(N)])
    if how == "apart": s = int(rng.integers(N * CAPP - CAP + 1)); cnt = np.bincount(np.repeat(np.arange(N), CAPP)[s:s + CAP], minlength=N); a = rng.permutation(N); O = np.stack([rng.permutation(np.repeat(np.arange(N), cnt[(a + k) % N])) for k in rng.permutation(N)])
    if how == "full": z = rng.permutation(N); O = np.stack([rng.permutation(np.repeat(z, CAPP)[:CAP]) for k in range(N)])
    if how == "none": z = int(rng.integers(N)); O = np.stack([rng.permutation(np.repeat(np.delete(np.arange(N), z), CAPP))[:CAP] for k in range(N)])
    P = np.zeros((N, CAP), np.int64)
    for o in range(N):
        q = rng.permutation(T); u = 0
        for k in range(N):
            m = np.nonzero(O[k] == o)[0]
            if how != "apart": q = rng.permutation(T); u = 0
            if how == "sorted": q = np.r_[0, T - 1, 1 + rng.permutation(T - 2)]
            P[k, m] = T * o + q[u:u + len(m)]; u += len(m)
    if how == "same": P = np.stack([rng.permutation(P[0]) for k in range(N)])
    if how == "sorted": P = np.sort(P, axis=1)
    G = 2 * rng.random((N, 16, CAP // 16), dtype=np.float32) - 1
    if how == "none": G[rng.random(G.shape) < 0.125] = 0
    return {"gate": G, "pick": np.stack([pack(p, 16) for p in P])}
def setup_inputs(rng):
    return dict({"x": rng.standard_normal((N, 128, T), dtype=np.float32), "w1": (rng.standard_normal((N, 128, FF * 128), dtype=np.float32) / 8), "w2": (rng.standard_normal((N, 128, FF * 128), dtype=np.float32) / 16)}, **lists(rng, "uniform"))
def setup_inputs_apart(rng):
    d = setup_inputs(rng); d.update(lists(rng, "apart"))
    for k in ("x",): d[k] = (d[k].astype(np.float32) * 1024.0).astype(d[k].dtype)
    return d
def setup_inputs_full(rng):
    d = setup_inputs(rng); d.update(lists(rng, "full"))
    for k in ("x",): d[k] = (d[k].astype(np.float32) * (1 / 1024.0)).astype(d[k].dtype)
    return d
def setup_inputs_none(rng):
    d = setup_inputs(rng); d.update(lists(rng, "none"))
    return d
def setup_inputs_same(rng):
    d = setup_inputs(rng); d.update(lists(rng, "same"))
    return d
def setup_inputs_sorted(rng):
    d = setup_inputs(rng); d.update(lists(rng, "sorted"))
    return d
def check_inputs(x):
    bad = []
    if x["pick"].min() < 0 or x["pick"].max() >= N * T: bad.append("pick out of range")
    if any(len(np.unique(a)) != a.size for a in x["pick"]): bad.append("a token stands twice in a list")
    if max(int(np.bincount(entries(a) // T, minlength=N).max()) for a in x["pick"]) > CAPP: bad.append("more than CAPP of an expert's tokens lie on one rank")
    return bad
def reference(x, w1, w2, gate, pick):
    X, W1, W2 = x.astype(np.float64), w1.astype(np.float64), w2.astype(np.float64)
    A = np.concatenate(list(X), axis=1); Y = np.zeros((128, N * T))
    for k in range(N):
        P = entries(pick[k]); g = entries(gate[k]).astype(np.float64)
        Y[:, P] += g[None, :] * sum(W2[k][:, 128 * f:128 * f + 128].T @ np.maximum(W1[k][:, 128 * f:128 * f + 128].T @ A[:, P], 0.0) for f in range(FF))
    return {"y": np.stack([Y[:, T * r:T * r + T] for r in range(N)]).astype(np.float32)}

@@ -1,0 +1,423 @@
+from concourse.bass import DstId, RemoteDMATransfer
+from concourse.mybir import AluOpType, ActivationFunctionType
+
+N, TOK, CAPP = 8, 4096, 256
+WIN = TOK + CAPP
+SIM_CORES = 256
+ZB = WIN // 8
+
+SCRATCH = {
+    "pk": ("sbuf", [128, 8], "int32"),
+    "wr": ("sbuf", [128, 528], "float32"),
+    "xw": ("sbuf", [128, WIN], "float32"),
+    "yw": ("sbuf", [128, WIN], "float32"),
+    "rid": ("sbuf", [128, 8], "int32"),
+    "tok": ("sbuf", [128, 8], "int32"),
+    "wtk": ("sbuf", [128, 8], "int32"),
+    "m64": ("sbuf", [128, 64], "bfloat16"),
+    "s64": ("sbuf", [128, 64], "bfloat16"),
+    "rst": ("sbuf", [128, 64], "bfloat16"),
+    "twor": ("sbuf", [128, 64], "bfloat16"),
+    "tt": ("sbuf", [128, 112], "float32"),
+    "posi": ("sbuf", [128, 8], "int32"),
+    "slot": ("sbuf", [128, 8], "int32"),
+    "ui": ("sbuf", [128, 8], "int32"),
+    "sci": ("sbuf", [128, 32], "int32"),
+    "scf": ("sbuf", [128, 32], "float32"),
+    "iom": ("sbuf", [128, 128], "bfloat16"),
+    "iob": ("sbuf", [128, 128], "bfloat16"),
+    "pci": ("sbuf", [128, 1], "int32"),
+    "pcm": ("sbuf", [128, 1], "int32"),
+    "pcf": ("sbuf", [128, 1], "float32"),
+    "cb": ("sbuf", [128, 128], "float32"),
+    "cc": ("sbuf", [128, 128], "float32"),
+    "lh": ("sbuf", [128, 1024], "bfloat16"),
+    "ra": ("sbuf", [128, 1024], "bfloat16"),
+    "rb": ("sbuf", [128, 1024], "bfloat16"),
+    "off": ("sbuf", [128, 128], "uint16"),
+    "lin": ("sbuf", [128, 112], "uint16"),
+    "tx": ("sbuf", [128, 8 * CAPP], "float32"),
+    "res": ("sbuf", [128, 8 * CAPP], "float32"),
+    "tmp": ("sbuf", [128, 8 * CAPP], "float32"),
+    "rel": ("sbuf", [128, 144], "float32"),
+    "wk": ("sbuf", [128, 512], "float32"),
+    "raw": ("sbuf", [128, 16], "float32"),
+    "xk": ("sbuf", [128, CAPP], "float32"),
+    "rk": ("sbuf", [128, CAPP], "float32"),
+    "mm": ("sbuf", [128, 24], "float32"),
+    "m8": ("sbuf", [128, 8], "bfloat16"),
+    "s8": ("sbuf", [128, 8], "bfloat16"),
+    "onb": ("sbuf", [128, 128], "bfloat16"),
+    "neb": ("sbuf", [128, 128], "bfloat16"),
+    "neg": ("sbuf", [128, 128], "bfloat16"),
+    "onf": ("sbuf", [128, 128], "float32"),
+    "idn": ("sbuf", [128, 128], "float32"),
+    "iof": ("sbuf", [128, 128], "float32"),
+    "gi": ("sbuf", [128, 8], "int32"),
+    "gsi": ("sbuf", [128, 16], "int32"),
+    "gsf": ("sbuf", [128, 16], "float32"),
+    "glh": ("sbuf", [128, 1024], "float32"),
+    "grg": ("sbuf", [128, 16], "float32"),
+    "gd": ("sbuf", [128, CAPP], "float32"),
+    "gr": ("sbuf", [128, CAPP], "float32"),
+    "h0": ("sbuf", [128, CAPP], "float32"),
+    "h1": ("sbuf", [128, CAPP], "float32"),
+    "pp": ("psum", [128, 512], "float32"),
+    "pl": ("psum", [128, 512], "float32"),
+    "pc": ("psum", [128, 512], "float32"),
+    "pg": ("psum", [128, 512], "float32"),
+    "ph0": ("psum", [128, 512], "float32"),
+    "ph1": ("psum", [128, 512], "float32"),
+    "po": ("psum", [128, 512], "float32"),
+}
+NEV = 110
+SEMAPHORES = (["sent", "rin", "rawin", "wA", "wB", "xin"] + ["l%d" % o for o in range(1, N)]
+              + ["r%d" % o for o in range(1, N)] + ["e%d" % i for i in range(NEV)])
+
+ADD, SUB, MUL, MAX = AluOpType.add, AluOpType.subtract, AluOpType.mult, AluOpType.max
+EQ, GE, GT = AluOpType.is_equal, AluOpType.is_ge, AluOpType.is_gt
+SHR, AND = AluOpType.arith_shift_right, AluOpType.bitwise_and
+RELU, COPY = ActivationFunctionType.Relu, ActivationFunctionType.Copy
+
+
+def chip_helpers(topo, rcore):
+    cs = [c for c in range(SIM_CORES)
+          if c != rcore and topo.host(c) == topo.host(rcore) and topo.chip(c) == topo.chip(rcore)]
+    return [c for c in cs if topo.die(c) != topo.die(rcore)] + [c for c in cs if topo.die(c) == topo.die(rcore)]
+
+
+def far_offsets(f):
+    a = [1 + (2 * f + i) % 7 for i in range(4)]
+    return a, [o for o in range(1, N) if o not in a]
+
+
+def rank_program(g, core, T, topo):
+    V, S, PE, SY = g.vector, g.scalar, g.tensor, g.sync
+    cores = T.cores
+    rank = T.rank_of(core)
+    home = None
+    for r in range(N):
+        if topo.host(cores[r]) == topo.host(core) and topo.chip(cores[r]) == topo.chip(core):
+            home = r
+    if home is None:
+        return
+    helpers = {r: chip_helpers(topo, cores[r]) for r in range(N)}
+
+    cnt = [0]
+    sent = [0]
+    events = []
+    done = {}
+
+    def ev():
+        e = [T.sem["e%d" % cnt[0]], 0, "e%d" % cnt[0], False]
+        cnt[0] += 1
+        events.append(e)
+        return e
+
+    def rem(name, n):
+        e = [T.sem[name], n, name, False]
+        events.append(e)
+        return e
+
+    def inc(ins, e, n=1):
+        ins.then_inc(e[0], n)
+        e[1] += n
+        return e
+
+    def one(ins, n=1):
+        return inc(ins, ev(), n)
+
+    def wait(q, *es):
+        qn = "v" if q is V else "s" if q is S else "p" if q is PE else "y" if q is SY else "g"
+        for e in es:
+            if done.get((qn, e[2])) != e[1]:
+                q.wait_ge(e[0], e[1])
+                done[(qn, e[2])] = e[1]
+                e[3] = True
+
+    def bits(dst):
+        m = topo.mask(core, dst)
+        return [b for b in range(16) if (m >> b) & 1]
+
+    def mk(bs):
+        return sum(1 << b for b in bs)
+
+    def did(dst):
+        rid, pid = topo.addr(dst, core)
+        return DstId(rid=rid, pnc=pid)
+
+    def xfer(src, dst, dests, sem, bs):
+        return RemoteDMATransfer(srcs=[src], dsts=[dst] * len(dests), dst_ids=[did(d) for d in dests],
+                                 dma_engine_mask=mk(bs), remote_sem=T.sem[sem])
+
+    def fused(trs, nb):
+        g.remote_dma_fused(trs, local_sem=T.sem.sent)
+        sent[0] += nb
+
+    def cols(t, c, w):
+        return t[:, c * w:(c + 1) * w]
+
+    def serves(k, o):
+        return helpers[(k - o) % N][o - 1]
+
+    def send_tile(f, offs, src, k):
+        ds = [serves(k, o) for o in offs]
+        b = bits(ds[0])
+        fused([xfer(src, cols(T.wk, f, 128), ds, "wA" if f < 2 else "wB", b)], len(b))
+
+    def factors_hot(e_gi, gate, e_gate, e_const):
+        wait(V, e_gi)
+        e1 = ev()
+        inc(V.tensor_scalar(T.gsi[:, 0:8], T.gi[:], 127, None, AND), e1)
+        inc(V.tensor_scalar(T.gsi[:, 8:16], T.gi[:], 7, None, SHR), e1)
+        wait(V, e1)
+        e2 = one(V.tensor_copy(T.gsf[:], T.gsi[:]))
+        wait(V, e2, e_const, *e_gate)
+        e3 = ev()
+        for c in range(8):
+            inc(V.tensor_scalar(cols(T.glh, c, 128), T.iof[:], T.gsf[:, c:c + 1], None, EQ), e3)
+            inc(V.tensor_scalar(cols(T.grg, c, 2), T.iof[:, 0:2], T.gsf[:, 8 + c:9 + c], gate[:, c:c + 1], EQ, MUL), e3)
+        wait(PE, e3)
+        for c in range(8):
+            m = PE.matmul(T.pc[:, 0:2], cols(T.glh, c, 128), cols(T.grg, c, 2), c == 0, c == 7)
+        return one(m)
+
+    def factors_row(e_col, e_idn, e_onf):
+        wait(V, e_col, e_idn)
+        e = ev()
+        for h in range(2):
+            inc(V.tensor_scalar(cols(T.gd, h, 128), T.idn[:], T.pc[:, h:h + 1], None, MUL), e)
+        wait(PE, e, e_onf)
+        e2 = one(PE.matmul(T.pg[:, 0:CAPP], T.onf[:], T.gd[:], True, True))
+        wait(S, e2)
+        return one(S.activation(T.gr[:], T.pg[:, 0:CAPP], COPY))
+
+    e_onb = one(V.memset(T.onb[:], 1.0))
+    e_neb = one(V.memset(T.neb[:], -1.0))
+    e_onf = one(V.memset(T.onf[:], 1.0))
+
+    if rank is None:
+        o = helpers[home].index(core) + 1
+        rcore = cores[home]
+        i = o - 1
+        wait(g, e_neb)
+        e_neg = one(g.affine_select(T.neg[:], T.neb[:], [[-1, 128]], GT, 0.0, 0, 1))
+        e_iof = one(g.iota(T.iof[:], [[1, 128]], 0, 0, allow_small_or_imprecise_dtypes=True))
+        wait(g, e_onf)
+        e_idn = one(g.affine_select(T.idn[:], T.onf[:], [[-1, 128]], EQ, 0.0, 0, 1))
+
+        if i < 4:
+            f, offs, n = i, far_offsets(i)[0], (4 if i < 2 else 2)
+        else:
+            f, n = (0, 1, 3)[i - 4], 4
+            offs = far_offsets(f)[1]
+        wait(g, rem("rin", n))
+        if i == 6:
+            ds = [serves(home, q) for q in range(1, N)]
+            b = bits(ds[0])
+            fused([xfer(T.rel[:, 128:144], T.raw[:], ds, "rawin", b)], len(b))
+        send_tile(f, offs, T.rel[:, 0:128], home)
+
+        e_raw = rem("rawin", 8)
+        wait(V, e_raw)
+        e = ev()
+        inc(V.tensor_scalar(T.mm[:, 0:8], T.raw[:, 0:8], float(TOK * home), None, GE), e)
+        inc(V.tensor_scalar(T.mm[:, 8:16], T.raw[:, 0:8], float(TOK * (home + 1)), None, GE), e)
+        wait(V, e)
+        e_m = one(V.tensor_tensor(T.m8[:], T.mm[:, 0:8], T.mm[:, 8:16], SUB))
+        wait(V, e_m, e_onb)
+        e_s = one(V.tensor_tensor_scan(T.s8[:], T.onb[:, 0:8], T.m8[:], 0.0, MUL, ADD))
+        wait(PE, e_s, e_m, e_onb, e_neg)
+        PE.matmul(T.pp[:, 0:8], T.onb[:], T.s8[:], True, False)
+        e_p = one(PE.matmul(T.pp[:, 0:8], T.neg[:], T.m8[:], False, True))
+        wait(V, e_p)
+        e_q = one(V.tensor_tensor(T.mm[:, 16:24], T.pp[:, 0:8], T.m8[:], MUL))
+        wait(V, e_q)
+        e_gi = one(V.tensor_scalar(T.gi[:], T.mm[:, 16:24], 1.0, None, SUB))
+        e_c = factors_hot(e_gi, T.raw[:, 8:16], [e_raw], e_iof)
+        e_g = factors_row(e_c, e_idn, e_onf)
+
+        w = T.wk
+        wait(PE, rem("wA", 16), rem("xin", 16 if o == 7 else 8))
+        e_a = one(PE.matmul(T.ph0[:, 0:CAPP], cols(w, 0, 128), T.xk[:], True, True))
+        e_b = one(PE.matmul(T.ph1[:, 0:CAPP], cols(w, 1, 128), T.xk[:], True, True))
+        wait(S, e_a)
+        e_h0 = one(S.activation(T.h0[:], T.ph0[:, 0:CAPP], RELU))
+        wait(V, e_b)
+        e_h1 = one(V.tensor_scalar(T.h1[:], T.ph1[:, 0:CAPP], 0.0, None, MAX))
+        wait(PE, rem("wB", 16), e_h0)
+        PE.matmul(T.po[:, 0:CAPP], cols(w, 2, 128), T.h0[:], True, False)
+        wait(PE, e_h1)
+        e_o = one(PE.matmul(T.po[:, 0:CAPP], cols(w, 3, 128), T.h1[:], False, True))
+        wait(V, e_o, e_g)
+        e_r = one(V.tensor_tensor(T.rk[:], T.po[:, 0:CAPP], T.gr[:], MUL))
+        wait(g, e_r)
+        b = bits(rcore)
+        fused([xfer(T.rk[:], cols(T.res, o, CAPP), [rcore], "r%d" % o, b)], len(b))
+    else:
+        r = rank
+        hs = helpers[r]
+        e_pk = one(SY.dma_start(T.pk[:], T.pick[:]), 16)
+        e_w1 = one(S.dma_start(T.wr[:, 0:256], T.w1[:]), 16)
+        e_w2 = one(SY.dma_start(T.wr[:, 256:512], T.w2[:]), 16)
+        e_gt = one(S.dma_start(T.wr[:, 520:528], T.gate[:]), 16)
+        e_x = one(SY.dma_start(T.xw[:, 0:TOK], T.x[:]), 16)
+
+        small = {"allow_small_or_imprecise_dtypes": True}
+        wait(g, e_onb)
+        e_rst = one(g.affine_select(T.rst[:], T.onb[:, 0:64], [[0, 8], [1, 8]], GT, 0.0, 0, 0))
+        e_two = one(g.iota(T.twor[:], [[2, 8], [0, 8]], 0, 0, **small))
+        wait(g, e_neb)
+        e_neg = one(g.affine_select(T.neg[:], T.neb[:], [[-1, 128]], GE, 0.0, 0, 1))
+        e_pci = one(g.iota(T.pci[:], [[0, 1]], 0, 1))
+        e_cb = one(g.iota(T.cb[:], [[0, 8], [16, 16]], TOK, 0, **small))
+        e_io = ev()
+        inc(g.iota(T.iom[:], [[0, 8], [1, 16]], 0, 0, **small), e_io)
+        inc(g.iota(T.iob[:], [[1, 128]], 0, 0, **small), e_io)
+        wait(g, e_onf)
+        e_idn = one(g.affine_select(T.idn[:], T.onf[:], [[-1, 128]], EQ, 0.0, 0, 1))
+        e_iof = one(g.iota(T.iof[:], [[1, 128]], 0, 0, **small))
+
+        e_zy = one(V.memset(T.yw[:, 0:ZB], 0.0))
+        e_zx = one(V.memset(T.xw[:, TOK:WIN], 0.0))
+        e_y0 = ev()
+        wait(S, e_zy)
+        for j in range(1, 8):
+            inc(S.activation(cols(T.yw, j, ZB), T.yw[:, 0:ZB], COPY), e_y0)
+
+        wait(V, e_pk)
+        e_rid = one(V.tensor_scalar(T.rid[:], T.pk[:], 12, None, SHR))
+        e_tok = one(V.tensor_scalar(T.tok[:], T.pk[:], TOK - 1, None, AND))
+        wait(V, e_rid)
+        e_m = ev()
+        for q in range(N):
+            inc(V.tensor_scalar(cols(T.m64, q, 8), T.rid[:], float(q), None, EQ), e_m)
+        wait(V, e_m, e_rst)
+        e_s = one(V.tensor_tensor_scan(T.s64[:], T.rst[:], T.m64[:], 0.0, MUL, ADD))
+        e_pf = one(V.tensor_copy(T.wr[:, 512:520], T.pk[:]))
+        wait(V, e_tok)
+        e_wtk = one(V.tensor_scalar(T.wtk[:], T.tok[:], -1.0, float(TOK), MUL, ADD))
+        wait(V, e_pci)
+        e_pcm = one(V.tensor_scalar(T.pcm[:], T.pci[:], 15, None, AND))
+        wait(PE, e_onb, e_two)
+        PE.matmul(T.pp[:, 0:64], T.onb[:], T.twor[:], True, False)
+        wait(PE, e_s, e_m, e_neg)
+        PE.matmul(T.pp[:, 0:64], T.onb[:], T.s64[:], False, False)
+        e_p = one(PE.matmul(T.pp[:, 0:64], T.neg[:], T.m64[:], False, True))
+        wait(V, e_pcm)
+        e_pcf = one(V.tensor_copy(T.pcf[:], T.pcm[:]))
+        wait(V, e_p)
+        e1 = one(V.tensor_tensor(T.tt[:, 0:64], T.pp[:, 0:64], T.m64[:], MUL))
+        wait(V, e1)
+        e1 = one(V.tensor_tensor(T.tt[:, 64:96], T.tt[:, 0:32], T.tt[:, 32:64], ADD))
+        wait(V, e1)
+        e1 = one(V.tensor_tensor(T.tt[:, 96:112], T.tt[:, 64:80], T.tt[:, 80:96], ADD))
+        wait(V, e_pcf, e_cb)
+        e_cc = one(V.tensor_scalar(T.cc[:], T.cb[:], T.pcf[:], None, ADD))
+        wait(V, e1)
+        e_pos = one(V.tensor_tensor(T.posi[:], T.tt[:, 96:104], T.tt[:, 104:112], ADD))
+        wait(PE, e_cc, e_idn)
+        PE.matmul(T.pl[:, 0:128], T.idn[:], T.cc[:], True, False)
+        wait(V, e_pos)
+        e_sl = one(V.tensor_scalar(T.slot[:], T.posi[:], CAPP - 1, None, AND))
+        e1 = ev()
+        inc(V.tensor_scalar(T.sci[:, 0:8], T.posi[:], 15, None, AND), e1)
+        inc(V.tensor_scalar(T.sci[:, 8:16], T.posi[:], 4, None, SHR), e1)
+        wait(V, e_sl, e_wtk)
+        e_u = one(V.tensor_tensor(T.ui[:], T.slot[:], T.wtk[:], ADD))
+        wait(V, e1)
+        e_f1 = one(V.tensor_copy(T.scf[:, 0:16], T.sci[:, 0:16]))
+        wait(V, e_u)
+        e2 = ev()
+        inc(V.tensor_scalar(T.sci[:, 16:24], T.ui[:], 8128, None, AND), e2)
+        inc(V.tensor_scalar(T.sci[:, 24:32], T.ui[:], 63, None, AND), e2)
+        wait(V, e2)
+        e_f2 = one(V.tensor_copy(T.scf[:, 16:32], T.sci[:, 16:32]))
+        wait(V, e_f1, e_io)
+        for c in range(8):
+            e = ev()
+            inc(V.tensor_scalar(cols(T.lh, c, 128), T.iom[:], T.scf[:, c:c + 1], -1.0, EQ, MUL), e)
+            wait(V, e_f2)
+            inc(V.tensor_scalar(cols(T.ra, c, 128), T.iob[:], T.scf[:, 8 + c:9 + c], T.scf[:, 16 + c:17 + c], EQ, MUL), e)
+            inc(V.tensor_scalar(cols(T.rb, c, 128), T.iob[:], T.scf[:, 8 + c:9 + c], T.scf[:, 24 + c:25 + c], EQ, MUL), e)
+            wait(PE, e)
+            PE.matmul(T.pl[:, 0:128], cols(T.lh, c, 128), cols(T.ra, c, 128), False, False)
+            m = PE.matmul(T.pl[:, 0:128], cols(T.lh, c, 128), cols(T.rb, c, 128), False, c == 7)
+        e_l = one(m)
+        e_gi = one(V.tensor_scalar(T.gi[:], T.posi[:], float(-CAPP * r), None, ADD))
+        wait(V, e_l)
+        e_off = one(V.tensor_copy(T.off[:], T.pl[:, 0:128]))
+
+        wait(g, e_w1, e_w2)
+        b = bits(hs[0])
+        fused([xfer(cols(T.wr, 0, 128), T.rel[:, 0:128], [hs[0], hs[4]], "rin", b[0:4]),
+               xfer(cols(T.wr, 1, 128), T.rel[:, 0:128], [hs[1], hs[5]], "rin", b[4:8]),
+               xfer(cols(T.wr, 2, 128), T.rel[:, 0:128], [hs[2]], "rin", b[8:10]),
+               xfer(cols(T.wr, 3, 128), T.rel[:, 0:128], [hs[3]], "rin", b[10:12])], 12)
+        wait(g, e_pf, e_gt)
+        fused([xfer(T.wr[:, 384:528], T.rel[:], [hs[6]], "rin", b[12:16])], 4)
+        send_tile(2, far_offsets(2)[1], cols(T.wr, 2, 128), r)
+
+        wait(g, e_off)
+        for grp in ((1, 2, 3, 4), (5, 6, 7)):
+            trs = []
+            for j, o in enumerate(grp):
+                d = cores[(r - o) % N]
+                trs.append(xfer(cols(T.off, (r - o) % N, 16), cols(T.lin, o - 1, 16), [d], "l%d" % o,
+                                bits(d)[2 * j:2 * j + 2]))
+            fused(trs, 2 * len(grp))
+
+        e_c = factors_hot(e_gi, T.wr[:, 520:528], [e_gt], e_iof)
+        own = T.off[:, 16 * r:16 * r + 16]
+        wait(V, e_off, e_x, e_zx)
+        e_t0 = one(V.tensor_copy(T.tx[:, 0:CAPP], T.xw[:].indirect(own)))
+        e_g = factors_row(e_c, e_idn, e_onf)
+        wait(PE, e_t0, e_w1, e_w2)
+        e_a = one(PE.matmul(T.ph0[:, 0:CAPP], cols(T.wr, 0, 128), T.tx[:, 0:CAPP], True, True))
+        e_b = one(PE.matmul(T.ph1[:, 0:CAPP], cols(T.wr, 1, 128), T.tx[:, 0:CAPP], True, True))
+        wait(S, e_a)
+        e_h0 = one(S.activation(T.h0[:], T.ph0[:, 0:CAPP], RELU))
+        wait(S, e_b)
+        e_h1 = one(S.activation(T.h1[:], T.ph1[:, 0:CAPP], RELU))
+        wait(PE, e_h0)
+        PE.matmul(T.po[:, 0:CAPP], cols(T.wr, 2, 128), T.h0[:], True, False)
+        wait(PE, e_h1)
+        e_o = one(PE.matmul(T.po[:, 0:CAPP], cols(T.wr, 3, 128), T.h1[:], False, True))
+
+        lists = {o: cols(T.lin, o - 1, 16) for o in range(1, N)}
+        el = {o: rem("l%d" % o, 2) for o in range(1, N)}
+        for grp in ((1, 2), (3, 4), (5, 6), (7,)):
+            es = []
+            for o in grp:
+                dst, src = cols(T.tx, o, CAPP), T.xw[:].indirect(lists[o])
+                if o % 2:
+                    wait(V, el[o])
+                    es.append(one(V.tensor_copy(dst, src)))
+                else:
+                    wait(S, el[o], e_x, e_zx)
+                    es.append(one(S.activation(dst, src, COPY)))
+            wait(g, *es)
+            trs = []
+            n = 16 // len(grp)
+            for j, o in enumerate(grp):
+                h = hs[o - 1]
+                trs.append(xfer(cols(T.tx, o, CAPP), T.xk[:], [h], "xin", bits(h)[n * j:n * j + n]))
+            fused(trs, 16)
+
+        wait(V, e_o, e_g)
+        e = one(V.tensor_tensor(T.res[:, 0:CAPP], T.po[:, 0:CAPP], T.gr[:], MUL))
+        wait(V, e, e_y0, e_zy)
+        e = one(V.tensor_copy(T.yw[:].indirect(own), T.res[:, 0:CAPP]))
+        for o in range(1, N):
+            wait(V, e, el[o], rem("r%d" % o, 16))
+            e = one(V.tensor_tensor(cols(T.tmp, o, CAPP), T.yw[:].indirect(lists[o]), cols(T.res, o, CAPP), ADD))
+            wait(V, e)
+            e = one(V.tensor_copy(T.yw[:].indirect(lists[o]), cols(T.tmp, o, CAPP)))
+        wait(SY, e)
+        e_y = one(SY.dma_start(T.y[:], T.yw[:, 0:TOK]), 16)
+        wait(SY, e_y)
+
+    for e in events:
+        if not e[3]:
+            wait(g, e)
+    g.wait_ge(T.sem.sent, sent[0])

@@ -2,93 +2,71 @@ from concourse.bass import DstId, RemoteDMATransfer
 from concourse.mybir import AluOpType, ActivationFunctionType
 
 N, TOK, CAPP = 8, 4096, 256
-WIN = TOK + CAPP
 SIM_CORES = 256
-ZB = WIN // 8
+Z = 16
+X0 = 1536
+PIECES = (512, 1024, 1024, 1536)
+
+F, I, B, U = "float32", "int32", "bfloat16", "uint16"
+
+
+def sb(n, dtype):
+    return ("sbuf", [128, n], dtype)
+
+
+SMALL = {}
+
+
+def pack(buf, items):
+    a = 0
+    for name, n in items:
+        SMALL[name] = (buf, a, n)
+        a += (n + 7) // 8 * 8
+    return a
+
+
+N_INT = pack("ints", [("rpi", 32), ("rbi", 16), ("tki", 8), ("lti", 16), ("gi", 8), ("gsi", 16), ("dsl", 32), ("dsi", 64),
+                      ("pci", 1), ("pcb", 2), ("rci", 16)])
+N_FLT = pack("flts", [("mm", 16), ("q", 8), ("tkf", 8), ("ltf", 16), ("gsf", 16), ("dsf", 64), ("pcf", 2), ("g1", 32),
+                      ("mx1", 128), ("mx2", 64), ("mx3", 32), ("lh", 128), ("rq", 128), ("rv", 128), ("rg", 128)])
 
 SCRATCH = {
-    "pk": ("sbuf", [128, 8], "int32"),
-    "wr": ("sbuf", [128, 528], "float32"),
-    "xw": ("sbuf", [128, WIN], "float32"),
-    "yw": ("sbuf", [128, WIN], "float32"),
-    "rid": ("sbuf", [128, 8], "int32"),
-    "tok": ("sbuf", [128, 8], "int32"),
-    "wtk": ("sbuf", [128, 8], "int32"),
-    "m64": ("sbuf", [128, 64], "bfloat16"),
-    "s64": ("sbuf", [128, 64], "bfloat16"),
-    "rst": ("sbuf", [128, 64], "bfloat16"),
-    "twor": ("sbuf", [128, 64], "bfloat16"),
-    "tt": ("sbuf", [128, 112], "float32"),
-    "posi": ("sbuf", [128, 8], "int32"),
-    "slot": ("sbuf", [128, 8], "int32"),
-    "ui": ("sbuf", [128, 8], "int32"),
-    "sci": ("sbuf", [128, 32], "int32"),
-    "scf": ("sbuf", [128, 32], "float32"),
-    "iom": ("sbuf", [128, 128], "bfloat16"),
-    "iob": ("sbuf", [128, 128], "bfloat16"),
-    "pci": ("sbuf", [128, 1], "int32"),
-    "pcm": ("sbuf", [128, 1], "int32"),
-    "pcf": ("sbuf", [128, 1], "float32"),
-    "cb": ("sbuf", [128, 128], "float32"),
-    "cc": ("sbuf", [128, 128], "float32"),
-    "lh": ("sbuf", [128, 1024], "bfloat16"),
-    "ra": ("sbuf", [128, 1024], "bfloat16"),
-    "rb": ("sbuf", [128, 1024], "bfloat16"),
-    "off": ("sbuf", [128, 128], "uint16"),
-    "lin": ("sbuf", [128, 112], "uint16"),
-    "tx": ("sbuf", [128, 8 * CAPP], "float32"),
-    "res": ("sbuf", [128, 8 * CAPP], "float32"),
-    "tmp": ("sbuf", [128, 8 * CAPP], "float32"),
-    "rel": ("sbuf", [128, 144], "float32"),
-    "wk": ("sbuf", [128, 512], "float32"),
-    "raw": ("sbuf", [128, 16], "float32"),
-    "xk": ("sbuf", [128, CAPP], "float32"),
-    "rk": ("sbuf", [128, CAPP], "float32"),
-    "mm": ("sbuf", [128, 24], "float32"),
-    "m8": ("sbuf", [128, 8], "bfloat16"),
-    "s8": ("sbuf", [128, 8], "bfloat16"),
-    "onb": ("sbuf", [128, 128], "bfloat16"),
-    "neb": ("sbuf", [128, 128], "bfloat16"),
-    "neg": ("sbuf", [128, 128], "bfloat16"),
-    "onf": ("sbuf", [128, 128], "float32"),
-    "idn": ("sbuf", [128, 128], "float32"),
-    "iof": ("sbuf", [128, 128], "float32"),
-    "gi": ("sbuf", [128, 8], "int32"),
-    "gsi": ("sbuf", [128, 16], "int32"),
-    "gsf": ("sbuf", [128, 16], "float32"),
-    "glh": ("sbuf", [128, 1024], "float32"),
-    "grg": ("sbuf", [128, 16], "float32"),
-    "gd": ("sbuf", [128, CAPP], "float32"),
-    "gr": ("sbuf", [128, CAPP], "float32"),
-    "h0": ("sbuf", [128, CAPP], "float32"),
-    "h1": ("sbuf", [128, CAPP], "float32"),
-    "pp": ("psum", [128, 512], "float32"),
-    "pl": ("psum", [128, 512], "float32"),
-    "pc": ("psum", [128, 512], "float32"),
-    "pg": ("psum", [128, 512], "float32"),
-    "ph0": ("psum", [128, 512], "float32"),
-    "ph1": ("psum", [128, 512], "float32"),
-    "po": ("psum", [128, 512], "float32"),
+    "ints": sb(N_INT, I), "flts": sb(N_FLT, F),
+    "pk": sb(8, I), "wr": sb(512, F), "xw": sb(TOK, F), "yw": sb(TOK, F),
+    "acc": sb(Z + N * CAPP, F), "res": sb(N * CAPP, F), "tx": sb(N * CAPP, F),
+    "lin": sb(N * 16, U), "pin": sb(N * 16, U), "repc": sb(16, U),
+    "mk0": sb(CAPP, F), "mki": sb(CAPP, F), "rlm": sb(128, F), "ivx": sb(CAPP, F), "inv": sb(CAPP, U),
+    "rel": sb(128, F), "rel2": sb(128, F), "rlx": sb(16, F),
+    "wk": sb(512, F), "xk": sb(CAPP, F), "rk": sb(CAPP, F), "gme": sb(32, F),
+    "pw": sb(16, F), "prv": sb(16, U), "lhs": sb(512, F), "rqs": sb(512, F), "rps": sb(512, F),
+    "raw": sb(16, F),
+    "onb": sb(128, B), "neb": sb(128, B), "neg": sb(128, B), "onf": sb(CAPP, F),
+    "rep": sb(32, U), "repb": sb(16, U),
+    "i16": sb(512, F), "i32": sb(CAPP, F), "i128": sb(128, B), "mk": sb(CAPP, F),
+    "m8": sb(8, B), "s8": sb(8, B),
+    "ow": sb(16, F), "off": sb(16, U), "gw": sb(16, F), "gd": sb(CAPP, F), "gr": sb(CAPP, F),
+    "lt": sb(1024, B), "rt": sb(CAPP, F), "rtv": sb(CAPP, B), "gt": sb(N * 32, F),
+    "h0": sb(CAPP, F), "h1": sb(CAPP, F),
 }
-NEV = 110
-SEMAPHORES = (["sent", "rin", "rawin", "wA", "wB", "xin"] + ["l%d" % o for o in range(1, N)]
-              + ["r%d" % o for o in range(1, N)] + ["e%d" % i for i in range(NEV)])
+for _n in ("pp", "pl", "pc", "pd", "pg", "ph0", "ph1", "po"):
+    SCRATCH[_n] = ("psum", [128, 512], "float32")
+NEV = 120
+SEMAPHORES = (["sent", "rin", "rlin", "rawin", "wA", "wB", "xin", "gin", "go"]
+              + [c + "%d" % o for c in "lpr" for o in range(1, N)] + ["e%d" % i for i in range(NEV)])
 
 ADD, SUB, MUL, MAX = AluOpType.add, AluOpType.subtract, AluOpType.mult, AluOpType.max
 EQ, GE, GT = AluOpType.is_equal, AluOpType.is_ge, AluOpType.is_gt
 SHR, AND = AluOpType.arith_shift_right, AluOpType.bitwise_and
 RELU, COPY = ActivationFunctionType.Relu, ActivationFunctionType.Copy
 
+SECOND = ((4, (5, 6, 7)), (5, (5, 6, 7)), (6, (6, 7)), (6, (5, 6, 7)))
+RAW1, RAW2 = (1, 2, 3, 4), (5, 6, 7)
+
 
 def chip_helpers(topo, rcore):
     cs = [c for c in range(SIM_CORES)
           if c != rcore and topo.host(c) == topo.host(rcore) and topo.chip(c) == topo.chip(rcore)]
     return [c for c in cs if topo.die(c) != topo.die(rcore)] + [c for c in cs if topo.die(c) == topo.die(rcore)]
-
-
-def far_offsets(f):
-    a = [1 + (2 * f + i) % 7 for i in range(4)]
-    return a, [o for o in range(1, N) if o not in a]
 
 
 def rank_program(g, core, T, topo):
@@ -102,7 +80,8 @@ def rank_program(g, core, T, topo):
     if home is None:
         return
     helpers = {r: chip_helpers(topo, cores[r]) for r in range(N)}
-
+    hs = helpers[home]
+    o = 0 if rank is not None else hs.index(core) + 1
     cnt = [0]
     sent = [0]
     events = []
@@ -135,12 +114,13 @@ def rank_program(g, core, T, topo):
                 done[(qn, e[2])] = e[1]
                 e[3] = True
 
+    def P(name, a=0, b=None):
+        buf, first, n = SMALL[name]
+        return T[buf][:, first + a:first + (n if b is None else b)]
+
     def bits(dst):
         m = topo.mask(core, dst)
         return [b for b in range(16) if (m >> b) & 1]
-
-    def mk(bs):
-        return sum(1 << b for b in bs)
 
     def did(dst):
         rid, pid = topo.addr(dst, core)
@@ -148,96 +128,210 @@ def rank_program(g, core, T, topo):
 
     def xfer(src, dst, dests, sem, bs):
         return RemoteDMATransfer(srcs=[src], dsts=[dst] * len(dests), dst_ids=[did(d) for d in dests],
-                                 dma_engine_mask=mk(bs), remote_sem=T.sem[sem])
+                                 dma_engine_mask=sum(1 << b for b in bs), remote_sem=T.sem[sem]), len(bs)
 
-    def fused(trs, nb):
-        g.remote_dma_fused(trs, local_sem=T.sem.sent)
-        sent[0] += nb
+    def fused(*trs):
+        g.remote_dma_fused([t for t, _ in trs], local_sem=T.sem.sent)
+        sent[0] += sum(n for _, n in trs)
 
     def cols(t, c, w):
         return t[:, c * w:(c + 1) * w]
 
-    def serves(k, o):
-        return helpers[(k - o) % N][o - 1]
+    def serves(k, q):
+        return helpers[(k - q) % N][q - 1]
 
-    def send_tile(f, offs, src, k):
-        ds = [serves(k, o) for o in offs]
-        b = bits(ds[0])
-        fused([xfer(src, cols(T.wk, f, 128), ds, "wA" if f < 2 else "wB", b)], len(b))
+    small = {"allow_small_or_imprecise_dtypes": True}
+    C = {}
 
-    def factors_hot(e_gi, gate, e_gate, e_const):
-        wait(V, e_gi)
-        e1 = ev()
-        inc(V.tensor_scalar(T.gsi[:, 0:8], T.gi[:], 127, None, AND), e1)
-        inc(V.tensor_scalar(T.gsi[:, 8:16], T.gi[:], 7, None, SHR), e1)
-        wait(V, e1)
-        e2 = one(V.tensor_copy(T.gsf[:], T.gsi[:]))
-        wait(V, e2, e_const, *e_gate)
-        e3 = ev()
-        for c in range(8):
-            inc(V.tensor_scalar(cols(T.glh, c, 128), T.iof[:], T.gsf[:, c:c + 1], None, EQ), e3)
-            inc(V.tensor_scalar(cols(T.grg, c, 2), T.iof[:, 0:2], T.gsf[:, 8 + c:9 + c], gate[:, c:c + 1], EQ, MUL), e3)
-        wait(PE, e3)
-        for c in range(8):
-            m = PE.matmul(T.pc[:, 0:2], cols(T.glh, c, 128), cols(T.grg, c, 2), c == 0, c == 7)
-        return one(m)
+    def consts_first():
+        wait(g, e_neb)
+        C["neg"] = one(g.affine_select(T.neg[:], T.neb[:], [[-1, 128]], GT, 0.0, 0, 1))
+        C["rpi"] = one(g.iota(P("rpi"), [[1, 32]], 0, 0))
+        w = 512 if o else 128
+        C["i16"] = one(g.iota(T.i16[:, 0:w], [[0, w // 16], [1, 16]], 0, 0, **small))
+        wait(V, C["rpi"])
+        C["rep"] = one(V.tensor_copy(T.rep[:], P("rpi")))
 
-    def factors_row(e_col, e_idn, e_onf):
-        wait(V, e_col, e_idn)
-        e = ev()
-        for h in range(2):
-            inc(V.tensor_scalar(cols(T.gd, h, 128), T.idn[:], T.pc[:, h:h + 1], None, MUL), e)
-        wait(PE, e, e_onf)
-        e2 = one(PE.matmul(T.pg[:, 0:CAPP], T.onf[:], T.gd[:], True, True))
-        wait(S, e2)
-        return one(S.activation(T.gr[:], T.pg[:, 0:CAPP], COPY))
+    def consts_rest():
+        C["rbi"] = one(g.iota(P("rbi"), [[1, 8], [0, 2]], 0, 0))
+        C["i128"] = one(g.iota(T.i128[:], [[1, 128]], 0, 0, **small))
+        C["i32"] = one(g.iota(T.i32[:], [[0, 8], [1, 32]], 0, 0, **small))
+        wait(g, e_onf)
+        C["mk"] = one(g.affine_select(T.mk[:], T.onf[:], [[0, 16], [1, 16]], EQ, 0.0, 0, -1))
 
     e_onb = one(V.memset(T.onb[:], 1.0))
     e_neb = one(V.memset(T.neb[:], -1.0))
     e_onf = one(V.memset(T.onf[:], 1.0))
+    e_gw0 = one(V.memset(T.gw[:], 0.0))
 
-    if rank is None:
-        o = helpers[home].index(core) + 1
-        rcore = cores[home]
-        i = o - 1
-        wait(g, e_neb)
-        e_neg = one(g.affine_select(T.neg[:], T.neb[:], [[-1, 128]], GT, 0.0, 0, 1))
-        e_iof = one(g.iota(T.iof[:], [[1, 128]], 0, 0, allow_small_or_imprecise_dtypes=True))
-        wait(g, e_onf)
-        e_idn = one(g.affine_select(T.idn[:], T.onf[:], [[-1, 128]], EQ, 0.0, 0, 1))
-
-        if i < 4:
-            f, offs, n = i, far_offsets(i)[0], (4 if i < 2 else 2)
-        else:
-            f, n = (0, 1, 3)[i - 4], 4
-            offs = far_offsets(f)[1]
-        wait(g, rem("rin", n))
-        if i == 6:
-            ds = [serves(home, q) for q in range(1, N)]
-            b = bits(ds[0])
-            fused([xfer(T.rel[:, 128:144], T.raw[:], ds, "rawin", b)], len(b))
-        send_tile(f, offs, T.rel[:, 0:128], home)
-
-        e_raw = rem("rawin", 8)
-        wait(V, e_raw)
+    def make_lists(e_pick, e_gate, own_table):
+        R = {}
+        pick, gate = T.raw[:, 0:8], T.raw[:, 8:16]
+        rp8 = T.rep[:, 0:8]
+        i16 = T.i16[:, 0:128]
+        wait(V, e_pick)
         e = ev()
-        inc(V.tensor_scalar(T.mm[:, 0:8], T.raw[:, 0:8], float(TOK * home), None, GE), e)
-        inc(V.tensor_scalar(T.mm[:, 8:16], T.raw[:, 0:8], float(TOK * (home + 1)), None, GE), e)
+        inc(V.tensor_scalar(P("mm", 0, 8), pick, float(TOK * home), None, GE), e)
+        inc(V.tensor_scalar(P("mm", 8, 16), pick, float(TOK * (home + 1)), None, GE), e)
+        e_tkf = one(V.tensor_scalar(P("tkf"), pick, float(-TOK * home), None, ADD))
         wait(V, e)
-        e_m = one(V.tensor_tensor(T.m8[:], T.mm[:, 0:8], T.mm[:, 8:16], SUB))
+        e_m = one(V.tensor_tensor(T.m8[:], P("mm", 0, 8), P("mm", 8, 16), SUB))
+        e_tki = one(V.tensor_scalar(P("tki"), pick, float(-TOK * home), None, ADD))
         wait(V, e_m, e_onb)
         e_s = one(V.tensor_tensor_scan(T.s8[:], T.onb[:, 0:8], T.m8[:], 0.0, MUL, ADD))
-        wait(PE, e_s, e_m, e_onb, e_neg)
+        wait(PE, e_s, e_m, e_onb, C["neg"])
         PE.matmul(T.pp[:, 0:8], T.onb[:], T.s8[:], True, False)
         e_p = one(PE.matmul(T.pp[:, 0:8], T.neg[:], T.m8[:], False, True))
+        wait(V, e_tki)
+        e_lti = ev()
+        inc(V.tensor_scalar(P("lti", 0, 8), P("tki"), 127, None, AND), e_lti)
+        inc(V.tensor_scalar(P("lti", 8, 16), P("tki"), 7, None, SHR), e_lti)
         wait(V, e_p)
-        e_q = one(V.tensor_tensor(T.mm[:, 16:24], T.pp[:, 0:8], T.m8[:], MUL))
+        e_q = one(V.tensor_tensor(P("q"), T.pp[:, 0:8], T.m8[:], MUL))
         wait(V, e_q)
-        e_gi = one(V.tensor_scalar(T.gi[:], T.mm[:, 16:24], 1.0, None, SUB))
-        e_c = factors_hot(e_gi, T.raw[:, 8:16], [e_raw], e_iof)
-        e_g = factors_row(e_c, e_idn, e_onf)
+        e_gi = one(V.tensor_scalar(P("gi"), P("q"), 1.0, None, SUB))
+        wait(V, e_gi)
+        e = ev()
+        inc(V.tensor_scalar(P("gsi", 0, 8), P("gi"), 15, None, AND), e)
+        inc(V.tensor_scalar(P("gsi", 8, 16), P("gi"), 4, None, SHR), e)
+        wait(V, e)
+        e_gsf = one(V.tensor_copy(P("gsf"), P("gsi")))
+        wait(V, e_gsf, C["rep"], C["i16"])
+        e_rq = one(V.tensor_tensor(P("rq"), P("gsf", 8, 16).indirect(rp8), i16, EQ))
+        e_lh = one(V.tensor_tensor(P("lh"), P("gsf", 0, 8).indirect(rp8), i16, EQ))
+        wait(V, e_rq, e_tkf)
+        e_rv = one(V.tensor_tensor(P("rv"), P("tkf").indirect(rp8), P("rq"), MUL))
+        wait(PE, e_lh, e_rv)
+        for c in range(8):
+            m = PE.matmul(T.pl[0:16, 0:16], P("lh", 16 * c, 16 * c + 16), P("rv", 16 * c, 16 * c + 16), c == 0, c == 7)
+        e_pl = one(m)
+        wait(V, *e_gate)
+        e_rg = one(V.tensor_tensor(P("rg"), gate.indirect(rp8), P("rq"), MUL))
+        wait(V, e_lti)
+        e_ltf = one(V.tensor_copy(P("ltf"), P("lti")))
+        wait(V, C["rbi"])
+        e_repb = one(V.tensor_copy(T.repb[:], P("rbi")))
+        wait(V, e_pl)
+        e_ow = one(V.tensor_copy(T.ow[0:16, :], T.pl[0:16, 0:16]))
+        wait(PE, e_ow, C["mk"])
+        e_pc = one(PE.matmul(T.pc[:, 0:16], T.mk[0:16, 0:128], T.ow[0:16, :], True, True))
+        wait(V, e_ltf, e_repb, C["i32"])
+        e_rt = one(V.tensor_tensor(T.rt[:], P("ltf", 8, 16).indirect(T.repb[:]), T.i32[:], EQ))
+        wait(V, e_pc)
+        R["off"] = one(V.tensor_copy(T.off[:], T.pc[:, 0:16]))
+        wait(V, e_rt, e_q)
+        e_rtv = one(V.tensor_tensor(T.rtv[:], P("q").indirect(T.repb[:]), T.rt[:], MUL))
+        wait(PE, e_rg, e_q)
+        for c in range(8):
+            m = PE.matmul(T.pp[0:16, 0:16], P("lh", 16 * c, 16 * c + 16), P("rg", 16 * c, 16 * c + 16), c == 0, c == 7)
+        e_pgt = one(m)
+        wait(V, C["i128"])
+        e_lt = ev()
+        for c in range(8):
+            inc(V.tensor_scalar(cols(T.lt, c, 128), T.i128[:], P("ltf", c, c + 1), None, EQ), e_lt)
+        wait(PE, e_lt, e_rtv)
+        for c in range(8):
+            m = PE.matmul(T.pd[:, 0:32], cols(T.lt, c, 128), cols(T.rtv, c, 32), c == 0, c == 7)
+        e_pd = one(m)
+        wait(V, e_pgt, e_gw0)
+        e_gw = one(V.tensor_copy(T.gw[0:16, :], T.pp[0:16, 0:16]))
+        wait(V, e_pd)
+        base = float(Z - 1 + CAPP * o)
+        e_g1 = one(V.tensor_scalar(P("g1"), T.pd[:, 0:32], 0.0, base, GT, MUL))
+        wait(V, e_g1)
+        R["g"] = one(V.tensor_tensor(own_table, T.pd[:, 0:32], P("g1"), ADD))
+        wait(V, e_gw, C["mk"])
+        e_gd = one(V.tensor_tensor(T.gd[:], T.gw[:].indirect(T.rep[:, 0:16]), T.mk[:], MUL))
+        wait(PE, e_gd, e_onf)
+        e_pg = one(PE.matmul(T.pg[:, 0:CAPP], T.onf[:, 0:128], T.gd[:], True, True))
+        wait(S, e_pg)
+        R["gr"] = one(S.activation(T.gr[:], T.pg[:, 0:CAPP], COPY))
+        R["ow"] = e_ow
+        return R
+
+    def largest(n, *es):
+        wait(V, *es)
+        left, right, e, w = T.gt[:, 0:128], T.gt[:, 128:256], None, 128
+        if n == 1:
+            return T.gt[:, 0:32], es
+        if n == 2:
+            e = one(V.tensor_tensor(P("mx3"), T.gt[:, 0:32], T.gt[:, 32:64], MAX))
+            return P("mx3"), (e,)
+        if n <= 4:
+            e = one(V.tensor_tensor(P("mx2"), T.gt[:, 0:64], T.gt[:, 64:128], MAX))
+        else:
+            e = one(V.tensor_tensor(P("mx1"), T.gt[:, 0:128], T.gt[:, 128:256], MAX))
+            wait(V, e)
+            e = one(V.tensor_tensor(P("mx2"), P("mx1", 0, 64), P("mx1", 64, 128), MAX))
+        wait(V, e)
+        e = one(V.tensor_tensor(P("mx3"), P("mx2", 0, 32), P("mx2", 32, 64), MAX))
+        return P("mx3"), (e,)
+
+    if rank is None:
+        rcore = cores[home]
+        i = o - 1
+        e_gt0 = one(V.memset(T.gt[:, 32 * o:N * 32], 0.0))
+        consts_first()
+        consts_rest()
+        if i == 6:
+            ds = [serves(home, q) for q in RAW2]
+            wait(g, rem("rlin", 8))
+            fused(xfer(T.rlx[:], T.raw[:], ds, "rawin", bits(ds[0])))
+        if i < 4:
+            h2, late = SECOND[i]
+            h2 = hs[h2]
+            ds = [serves(home, q) for q in range(1, N) if q not in late]
+            b = bits(ds[0])
+            wait(g, rem("rin", 4))
+            fused(xfer(T.rel[:], cols(T.wk, i, 128), ds, "wA" if i < 2 else "wB", b),
+                  xfer(T.rel[:], T.rel2[:] if i == 3 else T.rel[:], [h2], "rin", [q for q in bits(h2) if q not in b][:8]))
+        elif i < 6:
+            ds = [serves(home, q) for q in SECOND[i - 4][1]]
+            wait(g, rem("rin", 8))
+            fused(xfer(T.rel[:], cols(T.wk, i - 4, 128), ds, "wA", bits(ds[0])))
+        else:
+            d2, d3 = [[serves(home, q) for q in SECOND[f][1]] for f in (2, 3)]
+            b = bits(d2[0])
+            wait(g, rem("rin", 16))
+            fused(xfer(T.rel[:], cols(T.wk, 2, 128), d2, "wB", b[0:4]),
+                  xfer(T.rel2[:], cols(T.wk, 3, 128), d3, "wB", b[4:8]))
+
+        e_raw = rem("rawin", 8)
+        R = make_lists(e_raw, [e_raw], T.gme[:])
+        b = bits(rcore)
+        wait(g, R["off"])
+        fused(xfer(T.off[:], cols(T.lin, o, 16), [rcore], "l%d" % o, b))
+        wait(g, R["g"])
+        fused(xfer(T.gme[:], cols(T.gt, o, 32), hs[o:] + [rcore], "gin", b))
+
+        e_dsl = one(V.tensor_scalar(P("dsl"), T.pd[:, 0:32], 1.0, None, SUB))
+        wait(V, e_dsl)
+        e = ev()
+        inc(V.tensor_scalar(P("dsi", 0, 32), P("dsl"), 15, None, AND), e)
+        inc(V.tensor_scalar(P("dsi", 32, 64), P("dsl"), 4, None, SHR), e)
+        wait(V, e)
+        e_dsf = one(V.tensor_copy(P("dsf"), P("dsi")))
+        wait(V, e_dsf)
+        e_rqs = one(V.tensor_tensor(T.rqs[:], P("dsf", 32, 64).indirect(T.rep[:]), T.i16[:], EQ))
+        e_lhs = one(V.tensor_tensor(T.lhs[:], P("dsf", 0, 32).indirect(T.rep[:]), T.i16[:], EQ))
+        win, es = largest(o, rem("gin", 16 * o), e_gt0)
+        wait(V, e_rqs, *es)
+        e_rps = one(V.tensor_tensor(T.rps[:], win.indirect(T.rep[:]), T.rqs[:], MUL))
+        wait(PE, e_lhs, e_rps, R["ow"])
+        for c in range(32):
+            m = PE.matmul(T.pl[0:16, 0:16], cols(T.lhs, c, 16), cols(T.rps, c, 16), c == 0, c == 31)
+        e = one(m)
+        wait(V, e)
+        e_pw = one(V.tensor_copy(T.pw[0:16, :], T.pl[0:16, 0:16]))
+        wait(PE, e_pw, R["off"])
+        e = one(PE.matmul(T.pc[:, 0:16], T.mk[0:16, 0:128], T.pw[0:16, :], True, True))
+        wait(V, e)
+        e_prv = one(V.tensor_copy(T.prv[:], T.pc[:, 0:16]))
+        wait(g, e_prv)
+        fused(xfer(T.prv[:], cols(T.pin, o, 16), [rcore], "p%d" % o, b))
 
         w = T.wk
+        n_wb = sum(4 if o in SECOND[f][1] else 8 for f in (2, 3))
         wait(PE, rem("wA", 16), rem("xin", 16 if o == 7 else 8))
         e_a = one(PE.matmul(T.ph0[:, 0:CAPP], cols(w, 0, 128), T.xk[:], True, True))
         e_b = one(PE.matmul(T.ph1[:, 0:CAPP], cols(w, 1, 128), T.xk[:], True, True))
@@ -245,133 +339,69 @@ def rank_program(g, core, T, topo):
         e_h0 = one(S.activation(T.h0[:], T.ph0[:, 0:CAPP], RELU))
         wait(V, e_b)
         e_h1 = one(V.tensor_scalar(T.h1[:], T.ph1[:, 0:CAPP], 0.0, None, MAX))
-        wait(PE, rem("wB", 16), e_h0)
+        wait(PE, rem("wB", n_wb), e_h0)
         PE.matmul(T.po[:, 0:CAPP], cols(w, 2, 128), T.h0[:], True, False)
         wait(PE, e_h1)
         e_o = one(PE.matmul(T.po[:, 0:CAPP], cols(w, 3, 128), T.h1[:], False, True))
-        wait(V, e_o, e_g)
+        wait(V, e_o, R["gr"])
         e_r = one(V.tensor_tensor(T.rk[:], T.po[:, 0:CAPP], T.gr[:], MUL))
         wait(g, e_r)
-        b = bits(rcore)
-        fused([xfer(T.rk[:], cols(T.res, o, CAPP), [rcore], "r%d" % o, b)], len(b))
+        fused(xfer(T.rk[:], cols(T.res, o, CAPP), [rcore], "r%d" % o, b))
     else:
-        r = rank
-        hs = helpers[r]
         e_pk = one(SY.dma_start(T.pk[:], T.pick[:]), 16)
-        e_w1 = one(S.dma_start(T.wr[:, 0:256], T.w1[:]), 16)
-        e_w2 = one(SY.dma_start(T.wr[:, 256:512], T.w2[:]), 16)
-        e_gt = one(S.dma_start(T.wr[:, 520:528], T.gate[:]), 16)
-        e_x = one(SY.dma_start(T.xw[:, 0:TOK], T.x[:]), 16)
-
-        small = {"allow_small_or_imprecise_dtypes": True}
-        wait(g, e_onb)
-        e_rst = one(g.affine_select(T.rst[:], T.onb[:, 0:64], [[0, 8], [1, 8]], GT, 0.0, 0, 0))
-        e_two = one(g.iota(T.twor[:], [[2, 8], [0, 8]], 0, 0, **small))
-        wait(g, e_neb)
-        e_neg = one(g.affine_select(T.neg[:], T.neb[:], [[-1, 128]], GE, 0.0, 0, 1))
-        e_pci = one(g.iota(T.pci[:], [[0, 1]], 0, 1))
-        e_cb = one(g.iota(T.cb[:], [[0, 8], [16, 16]], TOK, 0, **small))
-        e_io = ev()
-        inc(g.iota(T.iom[:], [[0, 8], [1, 16]], 0, 0, **small), e_io)
-        inc(g.iota(T.iob[:], [[1, 128]], 0, 0, **small), e_io)
-        wait(g, e_onf)
-        e_idn = one(g.affine_select(T.idn[:], T.onf[:], [[-1, 128]], EQ, 0.0, 0, 1))
-        e_iof = one(g.iota(T.iof[:], [[1, 128]], 0, 0, **small))
-
-        e_zy = one(V.memset(T.yw[:, 0:ZB], 0.0))
-        e_zx = one(V.memset(T.xw[:, TOK:WIN], 0.0))
-        e_y0 = ev()
-        wait(S, e_zy)
-        for j in range(1, 8):
-            inc(S.activation(cols(T.yw, j, ZB), T.yw[:, 0:ZB], COPY), e_y0)
-
+        e_gt = one(S.dma_start(T.raw[:, 8:16], T.gate[:]), 16)
+        e_w1 = one(SY.dma_start(T.wr[:, 0:256], T.w1[:]), 16)
+        e_w2 = one(S.dma_start(T.wr[:, 256:512], T.w2[:]), 16)
+        e_x0 = one(SY.dma_start(T.xw[:, 0:X0], T.x[:, 0:X0]), 16)
+        e_z = one(V.memset(T.acc[:, 0:Z], 0.0))
+        consts_first()
         wait(V, e_pk)
-        e_rid = one(V.tensor_scalar(T.rid[:], T.pk[:], 12, None, SHR))
-        e_tok = one(V.tensor_scalar(T.tok[:], T.pk[:], TOK - 1, None, AND))
-        wait(V, e_rid)
-        e_m = ev()
-        for q in range(N):
-            inc(V.tensor_scalar(cols(T.m64, q, 8), T.rid[:], float(q), None, EQ), e_m)
-        wait(V, e_m, e_rst)
-        e_s = one(V.tensor_tensor_scan(T.s64[:], T.rst[:], T.m64[:], 0.0, MUL, ADD))
-        e_pf = one(V.tensor_copy(T.wr[:, 512:520], T.pk[:]))
-        wait(V, e_tok)
-        e_wtk = one(V.tensor_scalar(T.wtk[:], T.tok[:], -1.0, float(TOK), MUL, ADD))
-        wait(V, e_pci)
-        e_pcm = one(V.tensor_scalar(T.pcm[:], T.pci[:], 15, None, AND))
-        wait(PE, e_onb, e_two)
-        PE.matmul(T.pp[:, 0:64], T.onb[:], T.twor[:], True, False)
-        wait(PE, e_s, e_m, e_neg)
-        PE.matmul(T.pp[:, 0:64], T.onb[:], T.s64[:], False, False)
-        e_p = one(PE.matmul(T.pp[:, 0:64], T.neg[:], T.m64[:], False, True))
-        wait(V, e_pcm)
-        e_pcf = one(V.tensor_copy(T.pcf[:], T.pcm[:]))
-        wait(V, e_p)
-        e1 = one(V.tensor_tensor(T.tt[:, 0:64], T.pp[:, 0:64], T.m64[:], MUL))
-        wait(V, e1)
-        e1 = one(V.tensor_tensor(T.tt[:, 64:96], T.tt[:, 0:32], T.tt[:, 32:64], ADD))
-        wait(V, e1)
-        e1 = one(V.tensor_tensor(T.tt[:, 96:112], T.tt[:, 64:80], T.tt[:, 80:96], ADD))
-        wait(V, e_pcf, e_cb)
-        e_cc = one(V.tensor_scalar(T.cc[:], T.cb[:], T.pcf[:], None, ADD))
-        wait(V, e1)
-        e_pos = one(V.tensor_tensor(T.posi[:], T.tt[:, 96:104], T.tt[:, 104:112], ADD))
-        wait(PE, e_cc, e_idn)
-        PE.matmul(T.pl[:, 0:128], T.idn[:], T.cc[:], True, False)
-        wait(V, e_pos)
-        e_sl = one(V.tensor_scalar(T.slot[:], T.posi[:], CAPP - 1, None, AND))
-        e1 = ev()
-        inc(V.tensor_scalar(T.sci[:, 0:8], T.posi[:], 15, None, AND), e1)
-        inc(V.tensor_scalar(T.sci[:, 8:16], T.posi[:], 4, None, SHR), e1)
-        wait(V, e_sl, e_wtk)
-        e_u = one(V.tensor_tensor(T.ui[:], T.slot[:], T.wtk[:], ADD))
-        wait(V, e1)
-        e_f1 = one(V.tensor_copy(T.scf[:, 0:16], T.sci[:, 0:16]))
-        wait(V, e_u)
-        e2 = ev()
-        inc(V.tensor_scalar(T.sci[:, 16:24], T.ui[:], 8128, None, AND), e2)
-        inc(V.tensor_scalar(T.sci[:, 24:32], T.ui[:], 63, None, AND), e2)
-        wait(V, e2)
-        e_f2 = one(V.tensor_copy(T.scf[:, 16:32], T.sci[:, 16:32]))
-        wait(V, e_f1, e_io)
-        for c in range(8):
-            e = ev()
-            inc(V.tensor_scalar(cols(T.lh, c, 128), T.iom[:], T.scf[:, c:c + 1], -1.0, EQ, MUL), e)
-            wait(V, e_f2)
-            inc(V.tensor_scalar(cols(T.ra, c, 128), T.iob[:], T.scf[:, 8 + c:9 + c], T.scf[:, 16 + c:17 + c], EQ, MUL), e)
-            inc(V.tensor_scalar(cols(T.rb, c, 128), T.iob[:], T.scf[:, 8 + c:9 + c], T.scf[:, 24 + c:25 + c], EQ, MUL), e)
-            wait(PE, e)
-            PE.matmul(T.pl[:, 0:128], cols(T.lh, c, 128), cols(T.ra, c, 128), False, False)
-            m = PE.matmul(T.pl[:, 0:128], cols(T.lh, c, 128), cols(T.rb, c, 128), False, c == 7)
-        e_l = one(m)
-        e_gi = one(V.tensor_scalar(T.gi[:], T.posi[:], float(-CAPP * r), None, ADD))
-        wait(V, e_l)
-        e_off = one(V.tensor_copy(T.off[:], T.pl[:, 0:128]))
+        e_pf = one(V.tensor_copy(T.raw[:, 0:8], T.pk[:]))
 
+        ds = [serves(home, q) for q in RAW1]
+        b = bits(ds[0])
+        wait(g, e_pf, e_gt)
+        fused(xfer(T.raw[:], T.raw[:], ds, "rawin", b),
+              xfer(T.raw[:], T.rlx[:], [hs[6]], "rlin", [q for q in bits(hs[6]) if q not in b][:8]))
         wait(g, e_w1, e_w2)
         b = bits(hs[0])
-        fused([xfer(cols(T.wr, 0, 128), T.rel[:, 0:128], [hs[0], hs[4]], "rin", b[0:4]),
-               xfer(cols(T.wr, 1, 128), T.rel[:, 0:128], [hs[1], hs[5]], "rin", b[4:8]),
-               xfer(cols(T.wr, 2, 128), T.rel[:, 0:128], [hs[2]], "rin", b[8:10]),
-               xfer(cols(T.wr, 3, 128), T.rel[:, 0:128], [hs[3]], "rin", b[10:12])], 12)
-        wait(g, e_pf, e_gt)
-        fused([xfer(T.wr[:, 384:528], T.rel[:], [hs[6]], "rin", b[12:16])], 4)
-        send_tile(2, far_offsets(2)[1], cols(T.wr, 2, 128), r)
+        fused(*[xfer(cols(T.wr, f, 128), T.rel[:], [hs[f]], "rin", b[4 * f:4 * f + 4]) for f in range(4)])
+        g.sem_inc(T.sem.go, 1)
+        e_go = rem("go", 1)
+        wait(SY, e_go)
+        e_x1 = one(SY.dma_start(T.xw[:, X0:TOK], T.x[:, X0:TOK]), 16)
 
-        wait(g, e_off)
-        for grp in ((1, 2, 3, 4), (5, 6, 7)):
-            trs = []
-            for j, o in enumerate(grp):
-                d = cores[(r - o) % N]
-                trs.append(xfer(cols(T.off, (r - o) % N, 16), cols(T.lin, o - 1, 16), [d], "l%d" % o,
-                                bits(d)[2 * j:2 * j + 2]))
-            fused(trs, 2 * len(grp))
+        consts_rest()
+        R = make_lists(e_pf, [e_gt], T.gt[:, 0:32])
+        e_pci = one(g.iota(P("pci"), [[0, 1]], 0, 1))
+        e_rci = one(g.iota(P("rci"), [[2, 16]], 0, 0))
+        wait(g, R["g"])
+        fused(xfer(T.gt[:, 0:32], T.gt[:, 0:32], hs, "gin", bits(hs[0])))
+        e_k0 = one(g.affine_select(T.mk0[:], T.onf[:], [[0, 32], [-16, 8]], GE, 0.0, 0, 1))
+        wait(g, e_k0)
+        e_ki = one(g.affine_select(T.mki[:], T.mk0[:], [[0, 32], [16, 8]], GE, 0.0, 15, -1))
 
-        e_c = factors_hot(e_gi, T.wr[:, 520:528], [e_gt], e_iof)
-        own = T.off[:, 16 * r:16 * r + 16]
-        wait(V, e_off, e_x, e_zx)
-        e_t0 = one(V.tensor_copy(T.tx[:, 0:CAPP], T.xw[:].indirect(own)))
-        e_g = factors_row(e_c, e_idn, e_onf)
+        lists = {q: cols(T.lin, q, 16) for q in range(1, N)}
+        el = {q: rem("l%d" % q, 16) for q in range(1, N)}
+        wait(V, e_x0, e_x1)
+        wait(S, e_x0, e_x1)
+        for grp in ((1, 2), (3, 4), (5, 6), (7,)):
+            es = []
+            for q in grp:
+                dst, src = cols(T.tx, q, CAPP), T.xw[:].indirect(lists[q])
+                if q % 2:
+                    wait(V, el[q])
+                    es.append(one(V.tensor_copy(dst, src)))
+                else:
+                    wait(S, el[q])
+                    es.append(one(S.activation(dst, src, COPY)))
+            wait(g, *es)
+            n = 16 // len(grp)
+            fused(*[xfer(cols(T.tx, q, CAPP), T.xk[:], [hs[q - 1]], "xin", bits(hs[q - 1])[n * j:n * j + n])
+                    for j, q in enumerate(grp)])
+
+        wait(S, R["off"])
+        e_t0 = one(S.activation(T.tx[:, 0:CAPP], T.xw[:].indirect(T.off[:]), COPY))
         wait(PE, e_t0, e_w1, e_w2)
         e_a = one(PE.matmul(T.ph0[:, 0:CAPP], cols(T.wr, 0, 128), T.tx[:, 0:CAPP], True, True))
         e_b = one(PE.matmul(T.ph1[:, 0:CAPP], cols(T.wr, 1, 128), T.tx[:, 0:CAPP], True, True))
@@ -379,43 +409,47 @@ def rank_program(g, core, T, topo):
         e_h0 = one(S.activation(T.h0[:], T.ph0[:, 0:CAPP], RELU))
         wait(S, e_b)
         e_h1 = one(S.activation(T.h1[:], T.ph1[:, 0:CAPP], RELU))
+
+        wait(V, e_pci)
+        e = ev()
+        inc(V.tensor_scalar(P("pcb", 0, 1), P("pci"), 15, 3, AND, SHR), e)
+        inc(V.tensor_scalar(P("pcb", 1, 2), P("pci"), 15, None, AND), e)
+        wait(V, e)
+        e = one(V.tensor_copy(P("pcf"), P("pcb")))
+        wait(V, e, e_rci, C["i16"])
+        e_rpc = one(V.tensor_scalar(T.repc[:], P("rci"), P("pcf", 0, 1), None, ADD))
+        e_rlm = one(V.tensor_scalar(T.rlm[:], T.i16[:, 0:128], P("pcf", 1, 2), None, EQ))
+        win, es = largest(N, rem("gin", 16 * 7), R["g"])
+        wait(V, e_rpc, e_ki, *es)
+        e_ix = one(V.tensor_tensor(T.ivx[:], win.indirect(T.repc[:]), T.mki[:], MUL))
+        wait(PE, e_ix, e_rlm, R["ow"])
+        e = one(PE.matmul(T.pl[:, 0:CAPP], T.rlm[:], T.ivx[:], True, True))
+        wait(V, e)
+        e_inv = one(V.tensor_copy(T.inv[:], T.pl[:, 0:CAPP]))
+
         wait(PE, e_h0)
         PE.matmul(T.po[:, 0:CAPP], cols(T.wr, 2, 128), T.h0[:], True, False)
         wait(PE, e_h1)
         e_o = one(PE.matmul(T.po[:, 0:CAPP], cols(T.wr, 3, 128), T.h1[:], False, True))
 
-        lists = {o: cols(T.lin, o - 1, 16) for o in range(1, N)}
-        el = {o: rem("l%d" % o, 2) for o in range(1, N)}
-        for grp in ((1, 2), (3, 4), (5, 6), (7,)):
-            es = []
-            for o in grp:
-                dst, src = cols(T.tx, o, CAPP), T.xw[:].indirect(lists[o])
-                if o % 2:
-                    wait(V, el[o])
-                    es.append(one(V.tensor_copy(dst, src)))
-                else:
-                    wait(S, el[o], e_x, e_zx)
-                    es.append(one(S.activation(dst, src, COPY)))
-            wait(g, *es)
-            trs = []
-            n = 16 // len(grp)
-            for j, o in enumerate(grp):
-                h = hs[o - 1]
-                trs.append(xfer(cols(T.tx, o, CAPP), T.xk[:], [h], "xin", bits(h)[n * j:n * j + n]))
-            fused(trs, 16)
-
-        wait(V, e_o, e_g)
-        e = one(V.tensor_tensor(T.res[:, 0:CAPP], T.po[:, 0:CAPP], T.gr[:], MUL))
-        wait(V, e, e_y0, e_zy)
-        e = one(V.tensor_copy(T.yw[:].indirect(own), T.res[:, 0:CAPP]))
-        for o in range(1, N):
-            wait(V, e, el[o], rem("r%d" % o, 16))
-            e = one(V.tensor_tensor(cols(T.tmp, o, CAPP), T.yw[:].indirect(lists[o]), cols(T.res, o, CAPP), ADD))
-            wait(V, e)
-            e = one(V.tensor_copy(T.yw[:].indirect(lists[o]), cols(T.tmp, o, CAPP)))
-        wait(SY, e)
-        e_y = one(SY.dma_start(T.y[:], T.yw[:, 0:TOK]), 16)
-        wait(SY, e_y)
+        wait(V, e_o, R["gr"])
+        acc = [e_z, one(V.tensor_tensor(T.acc[:, Z:Z + CAPP], T.po[:, 0:CAPP], T.gr[:], MUL))]
+        for q in range(1, N):
+            wait(V, rem("p%d" % q, 16), rem("r%d" % q, 16), *acc)
+            lim = Z + CAPP * q
+            acc.append(one(V.tensor_tensor(T.acc[:, lim:lim + CAPP], T.acc[:, 0:lim].indirect(cols(T.pin, q, 16)),
+                                           cols(T.res, q, CAPP), ADD)))
+        wait(V, e_inv, *acc)
+        wait(S, e_inv, *acc)
+        es, a = [], 0
+        for n in PIECES:
+            h = a + n // 2
+            e1 = one(V.tensor_copy(T.yw[:, a:h], T.acc[:].indirect(T.inv[:, a // 16:h // 16])))
+            e2 = one(S.activation(T.yw[:, h:a + n], T.acc[:].indirect(T.inv[:, h // 16:(a + n) // 16]), COPY))
+            wait(SY, e1, e2)
+            es.append(one(SY.dma_start(T.y[:, a:a + n], T.yw[:, a:a + n]), 16))
+            a += n
+        wait(SY, *es)
 
     for e in events:
         if not e[3]:

@@ -4,10 +4,10 @@ from concourse.mybir import AluOpType, ActivationFunctionType
 N, TOK, CAPP = 8, 4096, 256
 SIM_CORES = 256
 Z = 16
-X0 = 1536
-PIECES = (512, 1024, 1024, 1536)
+X0 = 512
+PIECES = (256, 768, 1280, 1792)
 
-F, I, B, U = "float32", "int32", "bfloat16", "uint16"
+F, I, B, U, H = "float32", "int32", "bfloat16", "uint16", "float16"
 
 
 def sb(n, dtype):
@@ -27,7 +27,7 @@ def pack(buf, items):
 
 N_INT = pack("ints", [("rpi", 32), ("rbi", 16), ("tki", 8), ("lti", 16), ("gi", 8), ("gsi", 16), ("dsl", 32), ("dsi", 64),
                       ("pci", 1), ("pcb", 2), ("rci", 16)])
-N_FLT = pack("flts", [("mm", 16), ("q", 8), ("tkf", 8), ("ltf", 16), ("gsf", 16), ("dsf", 64), ("pcf", 2), ("g1", 32),
+N_FLT = pack("flts", [("mm", 16), ("q", 8), ("tkm", 8), ("gm", 8), ("ltf", 8), ("pcf", 2), ("g1", 32),
                       ("mx1", 128), ("mx2", 64), ("mx3", 32), ("lh", 128), ("rq", 128), ("rv", 128), ("rg", 128)])
 
 SCRATCH = {
@@ -37,15 +37,15 @@ SCRATCH = {
     "lin": sb(N * 16, U), "pin": sb(N * 16, U), "repc": sb(16, U),
     "mk0": sb(CAPP, F), "mki": sb(CAPP, F), "rlm": sb(128, F), "ivx": sb(CAPP, F), "inv": sb(CAPP, U),
     "rel": sb(128, F), "rel2": sb(128, F), "rlx": sb(16, F),
-    "wk": sb(512, F), "xk": sb(CAPP, F), "rk": sb(CAPP, F), "gme": sb(32, F),
-    "pw": sb(16, F), "prv": sb(16, U), "lhs": sb(512, F), "rqs": sb(512, F), "rps": sb(512, F),
+    "wk": sb(512, F), "xk": sb(CAPP, F), "rk": sb(CAPP, F), "gme": sb(32, F), "gms": sb(32, F),
+    "pw": sb(16, F), "prv": sb(16, U), "lhs": sb(512, H), "rqs": sb(512, H), "rps": sb(512, H),
     "raw": sb(16, F),
     "onb": sb(128, B), "neb": sb(128, B), "neg": sb(128, B), "onf": sb(CAPP, F),
     "rep": sb(32, U), "repb": sb(16, U),
     "i16": sb(512, F), "i32": sb(CAPP, F), "i128": sb(128, B), "mk": sb(CAPP, F),
     "m8": sb(8, B), "s8": sb(8, B),
     "ow": sb(16, F), "off": sb(16, U), "gw": sb(16, F), "gd": sb(CAPP, F), "gr": sb(CAPP, F),
-    "lt": sb(1024, B), "rt": sb(CAPP, F), "rtv": sb(CAPP, B), "gt": sb(N * 32, F),
+    "lta": sb(512, B), "lt": sb(1024, B), "rt": sb(CAPP, F), "rtv": sb(CAPP, B), "gt": sb(N * 32, F),
     "h0": sb(CAPP, F), "h1": sb(CAPP, F),
 }
 for _n in ("pp", "pl", "pc", "pd", "pg", "ph0", "ph1", "po"):
@@ -57,10 +57,11 @@ SEMAPHORES = (["sent", "rin", "rlin", "rawin", "wA", "wB", "xin", "gin", "go"]
 ADD, SUB, MUL, MAX = AluOpType.add, AluOpType.subtract, AluOpType.mult, AluOpType.max
 EQ, GE, GT = AluOpType.is_equal, AluOpType.is_ge, AluOpType.is_gt
 SHR, AND = AluOpType.arith_shift_right, AluOpType.bitwise_and
-RELU, COPY = ActivationFunctionType.Relu, ActivationFunctionType.Copy
+RELU, COPY, ABS = ActivationFunctionType.Relu, ActivationFunctionType.Copy, ActivationFunctionType.Abs
 
 SECOND = ((4, (5, 6, 7)), (5, (5, 6, 7)), (6, (6, 7)), (6, (5, 6, 7)))
-RAW1, RAW2 = (1, 2, 3, 4), (5, 6, 7)
+DIRECT = (1, 2, 3, 4, 5)
+RAW_RELAY = {4: (6,), 5: (7,)}
 
 
 def chip_helpers(topo, rcore):
@@ -122,6 +123,13 @@ def rank_program(g, core, T, topo):
         m = topo.mask(core, dst)
         return [b for b in range(16) if (m >> b) & 1]
 
+    off_chip = bits(cores[(home + 1) % N])
+
+    def chip_bits(dst):
+        return [b for b in bits(dst) if b not in off_chip]
+
+    NL = len(chip_bits(hs[o] if o == 0 else cores[home]))
+
     def did(dst):
         rid, pid = topo.addr(dst, core)
         return DstId(rid=rid, pnc=pid)
@@ -147,13 +155,15 @@ def rank_program(g, core, T, topo):
         wait(g, e_neb)
         C["neg"] = one(g.affine_select(T.neg[:], T.neb[:], [[-1, 128]], GT, 0.0, 0, 1))
         C["rpi"] = one(g.iota(P("rpi"), [[1, 32]], 0, 0))
+        C["rbi"] = one(g.iota(P("rbi"), [[1, 8], [0, 2]], 0, 0))
         w = 512 if o else 128
         C["i16"] = one(g.iota(T.i16[:, 0:w], [[0, w // 16], [1, 16]], 0, 0, **small))
         wait(V, C["rpi"])
         C["rep"] = one(V.tensor_copy(T.rep[:], P("rpi")))
+        wait(V, C["rbi"])
+        C["repb"] = one(V.tensor_copy(T.repb[:], P("rbi")))
 
     def consts_rest():
-        C["rbi"] = one(g.iota(P("rbi"), [[1, 8], [0, 2]], 0, 0))
         C["i128"] = one(g.iota(T.i128[:], [[1, 128]], 0, 0, **small))
         C["i32"] = one(g.iota(T.i32[:], [[0, 8], [1, 32]], 0, 0, **small))
         wait(g, e_onf)
@@ -173,7 +183,6 @@ def rank_program(g, core, T, topo):
         e = ev()
         inc(V.tensor_scalar(P("mm", 0, 8), pick, float(TOK * home), None, GE), e)
         inc(V.tensor_scalar(P("mm", 8, 16), pick, float(TOK * (home + 1)), None, GE), e)
-        e_tkf = one(V.tensor_scalar(P("tkf"), pick, float(-TOK * home), None, ADD))
         wait(V, e)
         e_m = one(V.tensor_tensor(T.m8[:], P("mm", 0, 8), P("mm", 8, 16), SUB))
         e_tki = one(V.tensor_scalar(P("tki"), pick, float(-TOK * home), None, ADD))
@@ -186,60 +195,64 @@ def rank_program(g, core, T, topo):
         e_lti = ev()
         inc(V.tensor_scalar(P("lti", 0, 8), P("tki"), 127, None, AND), e_lti)
         inc(V.tensor_scalar(P("lti", 8, 16), P("tki"), 7, None, SHR), e_lti)
+        e_tkm = one(V.tensor_tensor(P("tkm"), P("tki"), T.m8[:], MUL))
         wait(V, e_p)
-        e_q = one(V.tensor_tensor(P("q"), T.pp[:, 0:8], T.m8[:], MUL))
-        wait(V, e_q)
-        e_gi = one(V.tensor_scalar(P("gi"), P("q"), 1.0, None, SUB))
+        e_gi = one(V.tensor_scalar(P("gi"), T.pp[:, 0:8], 1.0, None, SUB))
+        e_q = one(V.tensor_copy(P("q"), T.pp[:, 0:8]))
         wait(V, e_gi)
-        e = ev()
-        inc(V.tensor_scalar(P("gsi", 0, 8), P("gi"), 15, None, AND), e)
-        inc(V.tensor_scalar(P("gsi", 8, 16), P("gi"), 4, None, SHR), e)
-        wait(V, e)
-        e_gsf = one(V.tensor_copy(P("gsf"), P("gsi")))
-        wait(V, e_gsf, C["rep"], C["i16"])
-        e_rq = one(V.tensor_tensor(P("rq"), P("gsf", 8, 16).indirect(rp8), i16, EQ))
-        e_lh = one(V.tensor_tensor(P("lh"), P("gsf", 0, 8).indirect(rp8), i16, EQ))
-        wait(V, e_rq, e_tkf)
-        e_rv = one(V.tensor_tensor(P("rv"), P("tkf").indirect(rp8), P("rq"), MUL))
+        e_gsi = ev()
+        inc(V.tensor_scalar(P("gsi", 8, 16), P("gi"), 4, None, SHR), e_gsi)
+        inc(V.tensor_scalar(P("gsi", 0, 8), P("gi"), 15, None, AND), e_gsi)
+        wait(V, e_lti)
+        e_ltf = one(V.tensor_scalar(P("ltf"), P("lti", 0, 8), -1.0, None, MUL))
+        wait(V, e_gsi, C["rep"], C["i16"])
+        e_rq = one(V.tensor_tensor(P("rq"), P("gsi", 8, 16).indirect(rp8), i16, EQ))
+        e_lh = one(V.tensor_tensor(P("lh"), P("gsi", 0, 8).indirect(rp8), i16, EQ))
+        wait(V, e_rq, e_tkm)
+        e_rv = one(V.tensor_tensor(P("rv"), P("tkm").indirect(rp8), P("rq"), MUL))
         wait(PE, e_lh, e_rv)
         for c in range(8):
             m = PE.matmul(T.pl[0:16, 0:16], P("lh", 16 * c, 16 * c + 16), P("rv", 16 * c, 16 * c + 16), c == 0, c == 7)
         e_pl = one(m)
+        wait(S, e_ltf, C["i128"])
+        e_lta = ev()
+        for c in range(4):
+            inc(S.activation(cols(T.lta, c, 128), T.i128[:], ABS, P("ltf", c, c + 1)), e_lta)
+        wait(S, e_lta)
+        e_lt = one(S.activation(T.lt[:, 0:512], T.lta[:], RELU, 1.0, -1.0))
+        wait(V, C["repb"], C["i32"])
+        e_rt = one(V.tensor_tensor(T.rt[:], P("lti", 8, 16).indirect(T.repb[:]), T.i32[:], EQ))
         wait(V, *e_gate)
-        e_rg = one(V.tensor_tensor(P("rg"), gate.indirect(rp8), P("rq"), MUL))
-        wait(V, e_lti)
-        e_ltf = one(V.tensor_copy(P("ltf"), P("lti")))
-        wait(V, C["rbi"])
-        e_repb = one(V.tensor_copy(T.repb[:], P("rbi")))
+        e_gm = one(V.tensor_tensor(P("gm"), gate, T.m8[:], MUL))
         wait(V, e_pl)
         e_ow = one(V.tensor_copy(T.ow[0:16, :], T.pl[0:16, 0:16]))
         wait(PE, e_ow, C["mk"])
         e_pc = one(PE.matmul(T.pc[:, 0:16], T.mk[0:16, 0:128], T.ow[0:16, :], True, True))
-        wait(V, e_ltf, e_repb, C["i32"])
-        e_rt = one(V.tensor_tensor(T.rt[:], P("ltf", 8, 16).indirect(T.repb[:]), T.i32[:], EQ))
+        wait(V, e_ltf, C["i128"])
+        e_lu = ev()
+        for c in range(4, 8):
+            inc(V.tensor_scalar(cols(T.lt, c, 128), T.i128[:], P("ltf", c, c + 1), 0.0, ADD, EQ), e_lu)
         wait(V, e_pc)
         R["off"] = one(V.tensor_copy(T.off[:], T.pc[:, 0:16]))
         wait(V, e_rt, e_q)
         e_rtv = one(V.tensor_tensor(T.rtv[:], P("q").indirect(T.repb[:]), T.rt[:], MUL))
-        wait(PE, e_rg, e_q)
-        for c in range(8):
-            m = PE.matmul(T.pp[0:16, 0:16], P("lh", 16 * c, 16 * c + 16), P("rg", 16 * c, 16 * c + 16), c == 0, c == 7)
-        e_pgt = one(m)
-        wait(V, C["i128"])
-        e_lt = ev()
-        for c in range(8):
-            inc(V.tensor_scalar(cols(T.lt, c, 128), T.i128[:], P("ltf", c, c + 1), None, EQ), e_lt)
-        wait(PE, e_lt, e_rtv)
+        wait(PE, e_lt, e_lu, e_rtv)
         for c in range(8):
             m = PE.matmul(T.pd[:, 0:32], cols(T.lt, c, 128), cols(T.rtv, c, 32), c == 0, c == 7)
         e_pd = one(m)
-        wait(V, e_pgt, e_gw0)
-        e_gw = one(V.tensor_copy(T.gw[0:16, :], T.pp[0:16, 0:16]))
+        wait(V, e_gm)
+        e_rg = one(V.tensor_tensor(P("rg"), P("gm").indirect(rp8), P("rq"), MUL))
+        wait(PE, e_rg, e_q, e_gi)
+        for c in range(8):
+            m = PE.matmul(T.pp[0:16, 0:16], P("lh", 16 * c, 16 * c + 16), P("rg", 16 * c, 16 * c + 16), c == 0, c == 7)
+        e_pgt = one(m)
         wait(V, e_pd)
         base = float(Z - 1 + CAPP * o)
         e_g1 = one(V.tensor_scalar(P("g1"), T.pd[:, 0:32], 0.0, base, GT, MUL))
         wait(V, e_g1)
         R["g"] = one(V.tensor_tensor(own_table, T.pd[:, 0:32], P("g1"), ADD))
+        wait(V, e_pgt, e_gw0)
+        e_gw = one(V.tensor_copy(T.gw[0:16, :], T.pp[0:16, 0:16]))
         wait(V, e_gw, C["mk"])
         e_gd = one(V.tensor_tensor(T.gd[:], T.gw[:].indirect(T.rep[:, 0:16]), T.mk[:], MUL))
         wait(PE, e_gd, e_onf)
@@ -251,12 +264,10 @@ def rank_program(g, core, T, topo):
 
     def largest(n, *es):
         wait(V, *es)
-        left, right, e, w = T.gt[:, 0:128], T.gt[:, 128:256], None, 128
         if n == 1:
             return T.gt[:, 0:32], es
         if n == 2:
-            e = one(V.tensor_tensor(P("mx3"), T.gt[:, 0:32], T.gt[:, 32:64], MAX))
-            return P("mx3"), (e,)
+            return T.gt[:, 32:64], es
         if n <= 4:
             e = one(V.tensor_tensor(P("mx2"), T.gt[:, 0:64], T.gt[:, 64:128], MAX))
         else:
@@ -271,38 +282,38 @@ def rank_program(g, core, T, topo):
         rcore = cores[home]
         i = o - 1
         e_gt0 = one(V.memset(T.gt[:, 32 * o:N * 32], 0.0))
+        if o > 1:
+            inc(V.memset(T.gt[:, 0:32], 0.0), e_gt0)
         consts_first()
         consts_rest()
-        if i == 6:
-            ds = [serves(home, q) for q in RAW2]
-            wait(g, rem("rlin", 8))
-            fused(xfer(T.rlx[:], T.raw[:], ds, "rawin", bits(ds[0])))
+        if i in RAW_RELAY:
+            wait(g, rem("rlin", NL))
+            fused(xfer(T.rlx[:], T.raw[:], [serves(home, q) for q in RAW_RELAY[i]], "rawin", off_chip))
         if i < 4:
             h2, late = SECOND[i]
             h2 = hs[h2]
             ds = [serves(home, q) for q in range(1, N) if q not in late]
-            b = bits(ds[0])
             wait(g, rem("rin", 4))
-            fused(xfer(T.rel[:], cols(T.wk, i, 128), ds, "wA" if i < 2 else "wB", b),
-                  xfer(T.rel[:], T.rel2[:] if i == 3 else T.rel[:], [h2], "rin", [q for q in bits(h2) if q not in b][:8]))
-        elif i < 6:
-            ds = [serves(home, q) for q in SECOND[i - 4][1]]
-            wait(g, rem("rin", 8))
-            fused(xfer(T.rel[:], cols(T.wk, i - 4, 128), ds, "wA", bits(ds[0])))
-        else:
-            d2, d3 = [[serves(home, q) for q in SECOND[f][1]] for f in (2, 3)]
-            b = bits(d2[0])
-            wait(g, rem("rin", 16))
-            fused(xfer(T.rel[:], cols(T.wk, 2, 128), d2, "wB", b[0:4]),
-                  xfer(T.rel2[:], cols(T.wk, 3, 128), d3, "wB", b[4:8]))
+            fused(xfer(T.rel[:], cols(T.wk, i, 128), ds, "wA" if i < 2 else "wB", off_chip),
+                  xfer(T.rel[:], T.rel2[:] if i == 3 else T.rel[:], [h2], "rin", chip_bits(h2)))
 
-        e_raw = rem("rawin", 8)
+        e_raw = rem("rawin", len(off_chip))
         R = make_lists(e_raw, [e_raw], T.gme[:])
-        b = bits(rcore)
+        lb = chip_bits(rcore)
         wait(g, R["off"])
-        fused(xfer(T.off[:], cols(T.lin, o, 16), [rcore], "l%d" % o, b))
-        wait(g, R["g"])
-        fused(xfer(T.gme[:], cols(T.gt, o, 32), hs[o:] + [rcore], "gin", b))
+        fused(xfer(T.off[:], cols(T.lin, o, 16), [rcore], "l%d" % o, lb))
+        if i == 6:
+            d2, d3 = [[serves(home, q) for q in SECOND[f][1]] for f in (2, 3)]
+            n = len(off_chip) // 2
+            wait(g, rem("rin", 2 * NL))
+            fused(xfer(T.rel[:], cols(T.wk, 2, 128), d2, "wB", off_chip[:n]),
+                  xfer(T.rel2[:], cols(T.wk, 3, 128), d3, "wB", off_chip[n:]))
+        elif i >= 4:
+            wait(g, rem("rin", NL))
+            fused(xfer(T.rel[:], cols(T.wk, i - 4, 128), [serves(home, q) for q in SECOND[i - 4][1]], "wA", off_chip))
+        if o > 1:
+            wait(g, R["g"])
+            fused(xfer(T.gme[:], cols(T.gt, o, 32), hs[o:] + [rcore], "gin", lb))
 
         e_dsl = one(V.tensor_scalar(P("dsl"), T.pd[:, 0:32], 1.0, None, SUB))
         wait(V, e_dsl)
@@ -310,11 +321,15 @@ def rank_program(g, core, T, topo):
         inc(V.tensor_scalar(P("dsi", 0, 32), P("dsl"), 15, None, AND), e)
         inc(V.tensor_scalar(P("dsi", 32, 64), P("dsl"), 4, None, SHR), e)
         wait(V, e)
-        e_dsf = one(V.tensor_copy(P("dsf"), P("dsi")))
-        wait(V, e_dsf)
-        e_rqs = one(V.tensor_tensor(T.rqs[:], P("dsf", 32, 64).indirect(T.rep[:]), T.i16[:], EQ))
-        e_lhs = one(V.tensor_tensor(T.lhs[:], P("dsf", 0, 32).indirect(T.rep[:]), T.i16[:], EQ))
-        win, es = largest(o, rem("gin", 16 * o), e_gt0)
+        e_rqs = one(V.tensor_tensor(T.rqs[:], P("dsi", 32, 64).indirect(T.rep[:]), T.i16[:], EQ))
+        e_lhs = one(V.tensor_tensor(T.lhs[:], P("dsi", 0, 32).indirect(T.rep[:]), T.i16[:], EQ))
+        e_gin = rem("gin", NL * max(1, o - 1))
+        if o == 1:
+            wait(V, e_gin, R["g"])
+            e = one(V.tensor_tensor(T.gms[:], T.gme[:], T.gt[:, 0:32], MAX))
+            wait(g, e)
+            fused(xfer(T.gms[:], cols(T.gt, o, 32), hs[o:] + [rcore], "gin", lb))
+        win, es = largest(o, e_gin, e_gt0)
         wait(V, e_rqs, *es)
         e_rps = one(V.tensor_tensor(T.rps[:], win.indirect(T.rep[:]), T.rqs[:], MUL))
         wait(PE, e_lhs, e_rps, R["ow"])
@@ -323,18 +338,19 @@ def rank_program(g, core, T, topo):
         e = one(m)
         wait(V, e)
         e_pw = one(V.tensor_copy(T.pw[0:16, :], T.pl[0:16, 0:16]))
+
+        w = T.wk
+        n_wb = sum(len(off_chip) // (2 if o in SECOND[f][1] else 1) for f in (2, 3))
+        b = bits(rcore)
+        wait(PE, rem("wA", 2 * len(off_chip)), rem("xin", len(b) if o == 7 else len(b) // 2))
+        e_a = one(PE.matmul(T.ph0[:, 0:CAPP], cols(w, 0, 128), T.xk[:], True, True))
         wait(PE, e_pw, R["off"])
         e = one(PE.matmul(T.pc[:, 0:16], T.mk[0:16, 0:128], T.pw[0:16, :], True, True))
+        e_b = one(PE.matmul(T.ph1[:, 0:CAPP], cols(w, 1, 128), T.xk[:], True, True))
         wait(V, e)
         e_prv = one(V.tensor_copy(T.prv[:], T.pc[:, 0:16]))
         wait(g, e_prv)
-        fused(xfer(T.prv[:], cols(T.pin, o, 16), [rcore], "p%d" % o, b))
-
-        w = T.wk
-        n_wb = sum(4 if o in SECOND[f][1] else 8 for f in (2, 3))
-        wait(PE, rem("wA", 16), rem("xin", 16 if o == 7 else 8))
-        e_a = one(PE.matmul(T.ph0[:, 0:CAPP], cols(w, 0, 128), T.xk[:], True, True))
-        e_b = one(PE.matmul(T.ph1[:, 0:CAPP], cols(w, 1, 128), T.xk[:], True, True))
+        fused(xfer(T.prv[:], cols(T.pin, o, 16), [rcore], "p%d" % o, lb))
         wait(S, e_a)
         e_h0 = one(S.activation(T.h0[:], T.ph0[:, 0:CAPP], RELU))
         wait(V, e_b)
@@ -358,17 +374,15 @@ def rank_program(g, core, T, topo):
         wait(V, e_pk)
         e_pf = one(V.tensor_copy(T.raw[:, 0:8], T.pk[:]))
 
-        ds = [serves(home, q) for q in RAW1]
-        b = bits(ds[0])
         wait(g, e_pf, e_gt)
-        fused(xfer(T.raw[:], T.raw[:], ds, "rawin", b),
-              xfer(T.raw[:], T.rlx[:], [hs[6]], "rlin", [q for q in bits(hs[6]) if q not in b][:8]))
+        fused(xfer(T.raw[:], T.raw[:], [serves(home, q) for q in DIRECT], "rawin", off_chip),
+              xfer(T.raw[:], T.rlx[:], [hs[h] for h in RAW_RELAY], "rlin", chip_bits(hs[0])))
         wait(g, e_w1, e_w2)
         b = bits(hs[0])
-        fused(*[xfer(cols(T.wr, f, 128), T.rel[:], [hs[f]], "rin", b[4 * f:4 * f + 4]) for f in range(4)])
+        order = chip_bits(hs[0]) + off_chip
+        fused(*[xfer(cols(T.wr, f, 128), T.rel[:], [hs[f]], "rin", order[4 * f:4 * f + 4]) for f in range(4)])
         g.sem_inc(T.sem.go, 1)
-        e_go = rem("go", 1)
-        wait(SY, e_go)
+        wait(SY, rem("go", 1))
         e_x1 = one(SY.dma_start(T.xw[:, X0:TOK], T.x[:, X0:TOK]), 16)
 
         consts_rest()
@@ -376,13 +390,13 @@ def rank_program(g, core, T, topo):
         e_pci = one(g.iota(P("pci"), [[0, 1]], 0, 1))
         e_rci = one(g.iota(P("rci"), [[2, 16]], 0, 0))
         wait(g, R["g"])
-        fused(xfer(T.gt[:, 0:32], T.gt[:, 0:32], hs, "gin", bits(hs[0])))
+        fused(xfer(T.gt[:, 0:32], T.gt[:, 0:32], [hs[0]], "gin", chip_bits(hs[0])))
         e_k0 = one(g.affine_select(T.mk0[:], T.onf[:], [[0, 32], [-16, 8]], GE, 0.0, 0, 1))
         wait(g, e_k0)
         e_ki = one(g.affine_select(T.mki[:], T.mk0[:], [[0, 32], [16, 8]], GE, 0.0, 15, -1))
 
         lists = {q: cols(T.lin, q, 16) for q in range(1, N)}
-        el = {q: rem("l%d" % q, 16) for q in range(1, N)}
+        el = {q: rem("l%d" % q, NL) for q in range(1, N)}
         wait(V, e_x0, e_x1)
         wait(S, e_x0, e_x1)
         for grp in ((1, 2), (3, 4), (5, 6), (7,)):
@@ -396,7 +410,7 @@ def rank_program(g, core, T, topo):
                     wait(S, el[q])
                     es.append(one(S.activation(dst, src, COPY)))
             wait(g, *es)
-            n = 16 // len(grp)
+            n = len(b) // len(grp)
             fused(*[xfer(cols(T.tx, q, CAPP), T.xk[:], [hs[q - 1]], "xin", bits(hs[q - 1])[n * j:n * j + n])
                     for j, q in enumerate(grp)])
 
@@ -419,7 +433,7 @@ def rank_program(g, core, T, topo):
         wait(V, e, e_rci, C["i16"])
         e_rpc = one(V.tensor_scalar(T.repc[:], P("rci"), P("pcf", 0, 1), None, ADD))
         e_rlm = one(V.tensor_scalar(T.rlm[:], T.i16[:, 0:128], P("pcf", 1, 2), None, EQ))
-        win, es = largest(N, rem("gin", 16 * 7), R["g"])
+        win, es = largest(N, rem("gin", NL * 7), R["g"])
         wait(V, e_rpc, e_ki, *es)
         e_ix = one(V.tensor_tensor(T.ivx[:], win.indirect(T.repc[:]), T.mki[:], MUL))
         wait(PE, e_ix, e_rlm, R["ow"])
@@ -435,7 +449,7 @@ def rank_program(g, core, T, topo):
         wait(V, e_o, R["gr"])
         acc = [e_z, one(V.tensor_tensor(T.acc[:, Z:Z + CAPP], T.po[:, 0:CAPP], T.gr[:], MUL))]
         for q in range(1, N):
-            wait(V, rem("p%d" % q, 16), rem("r%d" % q, 16), *acc)
+            wait(V, rem("p%d" % q, NL), rem("r%d" % q, len(b)), *acc)
             lim = Z + CAPP * q
             acc.append(one(V.tensor_tensor(T.acc[:, lim:lim + CAPP], T.acc[:, 0:lim].indirect(cols(T.pin, q, 16)),
                                            cols(T.res, q, CAPP), ADD)))

@@ -1,13 +1,14 @@
 from concourse.bass import DstId, RemoteDMATransfer
-from concourse.mybir import AluOpType, ActivationFunctionType
+from concourse.mybir import AluOpType, ActivationFunctionType, AxisListType
 
 N, TOK, CAPP = 8, 4096, 256
 SIM_CORES = 256
 Z = 16
 X0 = 512
-PIECES = (256, 768, 1280, 1792)
+BIG = 1024.0
+PIECES = (256, 640, 1024, 1280, 896)
 
-F, I, B, U, H = "float32", "int32", "bfloat16", "uint16", "float16"
+F, I, B, U = "float32", "int32", "bfloat16", "uint16"
 
 
 def sb(n, dtype):
@@ -25,9 +26,9 @@ def pack(buf, items):
     return a
 
 
-N_INT = pack("ints", [("rpi", 32), ("rbi", 16), ("tki", 8), ("lti", 16), ("gi", 8), ("gsi", 16), ("dsl", 32), ("dsi", 64),
-                      ("pci", 1), ("pcb", 2), ("rci", 16)])
-N_FLT = pack("flts", [("mm", 16), ("q", 8), ("tkm", 8), ("gm", 8), ("ltf", 8), ("pcf", 2), ("g1", 32),
+N_INT = pack("ints", [("rpi", 32), ("gi", 8), ("gsi", 16), ("tsi", 2), ("tqi", 4), ("pci", 1), ("pcb", 2), ("rci", 16)])
+N_FLT = pack("flts", [("mm", 16), ("tk1", 8), ("pcf", 2), ("m0", 16), ("m16", 16), ("pcn", 2), ("pcm", 16), ("tsf", 2),
+                      ("tqf", 4), ("mv", 64), ("m2", 64), ("prd", 64), ("pv", 2), ("rr", 16),
                       ("mx1", 128), ("mx2", 64), ("mx3", 32), ("lh", 128), ("rq", 128), ("rv", 128), ("rg", 128)])
 
 SCRATCH = {
@@ -36,16 +37,15 @@ SCRATCH = {
     "acc": sb(Z + N * CAPP, F), "res": sb(N * CAPP, F), "tx": sb(N * CAPP, F),
     "lin": sb(N * 16, U), "pin": sb(N * 16, U), "repc": sb(16, U),
     "mk0": sb(CAPP, F), "mki": sb(CAPP, F), "rlm": sb(128, F), "ivx": sb(CAPP, F), "inv": sb(CAPP, U),
-    "rel": sb(128, F), "rel2": sb(128, F), "rlx": sb(16, F),
+    "rel": sb(128, F), "rlx": sb(16, F),
     "wk": sb(512, F), "xk": sb(CAPP, F), "rk": sb(CAPP, F), "gme": sb(32, F), "gms": sb(32, F),
-    "pw": sb(16, F), "prv": sb(16, U), "lhs": sb(512, H), "rqs": sb(512, H), "rps": sb(512, H),
+    "prv": sb(16, U), "idn": sb(128, F), "lmt": sb(128, F), "t1": sb(CAPP, F),
     "raw": sb(16, F),
-    "onb": sb(128, B), "neb": sb(128, B), "neg": sb(128, B), "onf": sb(CAPP, F),
-    "rep": sb(32, U), "repb": sb(16, U),
-    "i16": sb(512, F), "i32": sb(CAPP, F), "i128": sb(128, B), "mk": sb(CAPP, F),
+    "onb": sb(128, B), "neb": sb(128, B), "ne0": sb(128, B), "neg": sb(128, B), "onf": sb(CAPP, F),
+    "rep": sb(32, U), "i16": sb(128, F), "i128": sb(128, F), "mk": sb(CAPP, F),
     "m8": sb(8, B), "s8": sb(8, B),
     "ow": sb(16, F), "off": sb(16, U), "gw": sb(16, F), "gd": sb(CAPP, F), "gr": sb(CAPP, F),
-    "lta": sb(512, B), "lt": sb(1024, B), "rt": sb(CAPP, F), "rtv": sb(CAPP, B), "gt": sb(N * 32, F),
+    "oh": sb(CAPP, F), "gt": sb(N * 32, F),
     "h0": sb(CAPP, F), "h1": sb(CAPP, F),
 }
 for _n in ("pp", "pl", "pc", "pd", "pg", "ph0", "ph1", "po"):
@@ -55,13 +55,15 @@ SEMAPHORES = (["sent", "rin", "rlin", "rawin", "wA", "wB", "xin", "gin", "go"]
               + [c + "%d" % o for c in "lpr" for o in range(1, N)] + ["e%d" % i for i in range(NEV)])
 
 ADD, SUB, MUL, MAX = AluOpType.add, AluOpType.subtract, AluOpType.mult, AluOpType.max
-EQ, GE, GT = AluOpType.is_equal, AluOpType.is_ge, AluOpType.is_gt
+EQ, NE, GE, GT = AluOpType.is_equal, AluOpType.not_equal, AluOpType.is_ge, AluOpType.is_gt
 SHR, AND = AluOpType.arith_shift_right, AluOpType.bitwise_and
-RELU, COPY, ABS = ActivationFunctionType.Relu, ActivationFunctionType.Copy, ActivationFunctionType.Abs
+RELU, COPY = ActivationFunctionType.Relu, ActivationFunctionType.Copy
+AX = AxisListType.X
 
-SECOND = ((4, (5, 6, 7)), (5, (5, 6, 7)), (6, (6, 7)), (6, (5, 6, 7)))
+RELAY = (0, 4, 2, 6)
 DIRECT = (1, 2, 3, 4, 5)
-RAW_RELAY = {4: (6,), 5: (7,)}
+RAW_RELAY = {3: (6,), 5: (7,)}
+GROUPS = ((1,), (2,), (3, 4), (5, 6), (7,))
 
 
 def chip_helpers(topo, rcore):
@@ -152,25 +154,32 @@ def rank_program(g, core, T, topo):
     C = {}
 
     def consts_first():
-        wait(g, e_neb)
-        C["neg"] = one(g.affine_select(T.neg[:], T.neb[:], [[-1, 128]], GT, 0.0, 0, 1))
         C["rpi"] = one(g.iota(P("rpi"), [[1, 32]], 0, 0))
-        C["rbi"] = one(g.iota(P("rbi"), [[1, 8], [0, 2]], 0, 0))
-        w = 512 if o else 128
-        C["i16"] = one(g.iota(T.i16[:, 0:w], [[0, w // 16], [1, 16]], 0, 0, **small))
+        wait(g, e_neb)
+        C["ne0"] = one(g.affine_select(T.ne0[:], T.neb[:], [[-1, 128]], GT, 0.0, 0, 1))
         wait(V, C["rpi"])
         C["rep"] = one(V.tensor_copy(T.rep[:], P("rpi")))
-        wait(V, C["rbi"])
-        C["repb"] = one(V.tensor_copy(T.repb[:], P("rbi")))
 
-    def consts_rest():
-        C["i128"] = one(g.iota(T.i128[:], [[1, 128]], 0, 0, **small))
-        C["i32"] = one(g.iota(T.i32[:], [[0, 8], [1, 32]], 0, 0, **small))
+    def consts_neg():
+        wait(g, C["ne0"])
+        C["neg"] = one(g.affine_select(T.neg[:], T.ne0[:], [[-1, 128]], NE, BIG, 0, 1))
+
+    def consts_mid():
+        C["i16"] = one(g.iota(T.i16[:], [[0, 8], [1, 16]], 0, 0, **small))
         wait(g, e_onf)
+        C["m0"] = one(g.affine_select(P("m0"), T.onf[:, 0:16], [[0, 2], [-16, 8]], GE, 0.0, 0, 1))
         C["mk"] = one(g.affine_select(T.mk[:], T.onf[:], [[0, 16], [1, 16]], EQ, 0.0, 0, -1))
 
-    e_onb = one(V.memset(T.onb[:], 1.0))
+    def consts_rest():
+        wait(g, C["m0"])
+        C["m16"] = one(g.affine_select(P("m16"), P("m0"), [[0, 2], [16, 8]], GE, 0.0, 15, -1))
+        C["i128"] = one(g.iota(T.i128[:], [[1, 128]], 0, 0, **small))
+        C["pcn"] = one(g.iota(P("pcn"), [[128, 2]], Z + CAPP * o, 1, **small))
+        if o:
+            C["idn"] = one(g.affine_select(T.idn[:], T.onf[:, 0:128], [[-1, 128]], EQ, 0.0, 0, 1))
+
     e_neb = one(V.memset(T.neb[:], -1.0))
+    e_onb = one(V.memset(T.onb[:], 1.0))
     e_onf = one(V.memset(T.onf[:], 1.0))
     e_gw0 = one(V.memset(T.gw[:], 0.0))
 
@@ -178,88 +187,91 @@ def rank_program(g, core, T, topo):
         R = {}
         pick, gate = T.raw[:, 0:8], T.raw[:, 8:16]
         rp8 = T.rep[:, 0:8]
-        i16 = T.i16[:, 0:128]
         wait(V, e_pick)
         e = ev()
         inc(V.tensor_scalar(P("mm", 0, 8), pick, float(TOK * home), None, GE), e)
         inc(V.tensor_scalar(P("mm", 8, 16), pick, float(TOK * (home + 1)), None, GE), e)
         wait(V, e)
         e_m = one(V.tensor_tensor(T.m8[:], P("mm", 0, 8), P("mm", 8, 16), SUB))
-        e_tki = one(V.tensor_scalar(P("tki"), pick, float(-TOK * home), None, ADD))
+        e_tk = one(V.tensor_scalar(P("tk1"), pick, float(1 - TOK * home), None, ADD))
         wait(V, e_m, e_onb)
         e_s = one(V.tensor_tensor_scan(T.s8[:], T.onb[:, 0:8], T.m8[:], 0.0, MUL, ADD))
         wait(PE, e_s, e_m, e_onb, C["neg"])
         PE.matmul(T.pp[:, 0:8], T.onb[:], T.s8[:], True, False)
         e_p = one(PE.matmul(T.pp[:, 0:8], T.neg[:], T.m8[:], False, True))
-        wait(V, e_tki)
-        e_lti = ev()
-        inc(V.tensor_scalar(P("lti", 0, 8), P("tki"), 127, None, AND), e_lti)
-        inc(V.tensor_scalar(P("lti", 8, 16), P("tki"), 7, None, SHR), e_lti)
-        e_tkm = one(V.tensor_tensor(P("tkm"), P("tki"), T.m8[:], MUL))
         wait(V, e_p)
-        e_gi = one(V.tensor_scalar(P("gi"), T.pp[:, 0:8], 1.0, None, SUB))
-        e_q = one(V.tensor_copy(P("q"), T.pp[:, 0:8]))
+        e_gi = one(V.tensor_scalar(P("gi"), T.pp[:, 0:8], BIG + 1.0, None, SUB))
         wait(V, e_gi)
         e_gsi = ev()
         inc(V.tensor_scalar(P("gsi", 8, 16), P("gi"), 4, None, SHR), e_gsi)
         inc(V.tensor_scalar(P("gsi", 0, 8), P("gi"), 15, None, AND), e_gsi)
-        wait(V, e_lti)
-        e_ltf = one(V.tensor_scalar(P("ltf"), P("lti", 0, 8), -1.0, None, MUL))
         wait(V, e_gsi, C["rep"], C["i16"])
-        e_rq = one(V.tensor_tensor(P("rq"), P("gsi", 8, 16).indirect(rp8), i16, EQ))
-        e_lh = one(V.tensor_tensor(P("lh"), P("gsi", 0, 8).indirect(rp8), i16, EQ))
-        wait(V, e_rq, e_tkm)
-        e_rv = one(V.tensor_tensor(P("rv"), P("tkm").indirect(rp8), P("rq"), MUL))
+        e_rq = one(V.tensor_tensor(P("rq"), P("gsi", 8, 16).indirect(rp8), T.i16[:], EQ))
+        e_lh = one(V.tensor_tensor(P("lh"), P("gsi", 0, 8).indirect(rp8), T.i16[:], EQ))
+        wait(V, e_rq, e_tk)
+        e_rv = one(V.tensor_tensor(P("rv"), P("tk1").indirect(rp8), P("rq"), MUL))
         wait(PE, e_lh, e_rv)
         for c in range(8):
             m = PE.matmul(T.pl[0:16, 0:16], P("lh", 16 * c, 16 * c + 16), P("rv", 16 * c, 16 * c + 16), c == 0, c == 7)
         e_pl = one(m)
-        wait(S, e_ltf, C["i128"])
-        e_lta = ev()
-        for c in range(4):
-            inc(S.activation(cols(T.lta, c, 128), T.i128[:], ABS, P("ltf", c, c + 1)), e_lta)
-        wait(S, e_lta)
-        e_lt = one(S.activation(T.lt[:, 0:512], T.lta[:], RELU, 1.0, -1.0))
-        wait(V, C["repb"], C["i32"])
-        e_rt = one(V.tensor_tensor(T.rt[:], P("lti", 8, 16).indirect(T.repb[:]), T.i32[:], EQ))
         wait(V, *e_gate)
-        e_gm = one(V.tensor_tensor(P("gm"), gate, T.m8[:], MUL))
+        e_rg = one(V.tensor_tensor(P("rg"), gate.indirect(rp8), P("rq"), MUL))
         wait(V, e_pl)
-        e_ow = one(V.tensor_copy(T.ow[0:16, :], T.pl[0:16, 0:16]))
-        wait(PE, e_ow, C["mk"])
+        R["ow"] = one(V.tensor_copy(T.ow[0:16, :], T.pl[0:16, 0:16]))
+        wait(PE, R["ow"], C["mk"])
         e_pc = one(PE.matmul(T.pc[:, 0:16], T.mk[0:16, 0:128], T.ow[0:16, :], True, True))
-        wait(V, e_ltf, C["i128"])
-        e_lu = ev()
-        for c in range(4, 8):
-            inc(V.tensor_scalar(cols(T.lt, c, 128), T.i128[:], P("ltf", c, c + 1), 0.0, ADD, EQ), e_lu)
-        wait(V, e_pc)
-        R["off"] = one(V.tensor_copy(T.off[:], T.pc[:, 0:16]))
-        wait(V, e_rt, e_q)
-        e_rtv = one(V.tensor_tensor(T.rtv[:], P("q").indirect(T.repb[:]), T.rt[:], MUL))
-        wait(PE, e_lt, e_lu, e_rtv)
-        for c in range(8):
-            m = PE.matmul(T.pd[:, 0:32], cols(T.lt, c, 128), cols(T.rtv, c, 32), c == 0, c == 7)
-        e_pd = one(m)
-        wait(V, e_gm)
-        e_rg = one(V.tensor_tensor(P("rg"), P("gm").indirect(rp8), P("rq"), MUL))
-        wait(PE, e_rg, e_q, e_gi)
+        wait(PE, e_rg, e_gi)
         for c in range(8):
             m = PE.matmul(T.pp[0:16, 0:16], P("lh", 16 * c, 16 * c + 16), P("rg", 16 * c, 16 * c + 16), c == 0, c == 7)
         e_pgt = one(m)
-        wait(V, e_pd)
-        base = float(Z - 1 + CAPP * o)
-        e_g1 = one(V.tensor_scalar(P("g1"), T.pd[:, 0:32], 0.0, base, GT, MUL))
-        wait(V, e_g1)
-        R["g"] = one(V.tensor_tensor(own_table, T.pd[:, 0:32], P("g1"), ADD))
+        wait(V, e_pc)
+        R["off"] = one(V.tensor_scalar(T.off[:], T.pc[:, 0:16], 1.0, None, SUB))
+        wait(V, C["m16"])
+        e = one(V.tensor_tensor(P("pcm"), T.pc[:, 0:16], P("m16"), MUL))
+        wait(V, e)
+        e = ev()
+        for c in range(2):
+            inc(V.tensor_reduce(P("tsf", c, c + 1), P("pcm", 8 * c, 8 * c + 8), AX, ADD), e)
+        wait(V, e)
+        e = one(V.tensor_scalar(P("tsi"), P("tsf"), 1.0, None, SUB))
+        wait(V, e)
+        e = ev()
+        inc(V.tensor_scalar(P("tqi", 0, 2), P("tsi"), 127, None, AND), e)
+        inc(V.tensor_scalar(P("tqi", 2, 4), P("tsi"), 7, None, SHR), e)
+        wait(V, e)
+        e = one(V.tensor_copy(P("tqf"), P("tqi")))
+        wait(V, e, C["i128"], C["pcn"])
+        e_oh = ev()
+        for c in range(2):
+            inc(V.tensor_scalar(P("mv", 32 * c, 32 * c + 32), T.i128[:, 0:32], P("tqf", 2 + c, 3 + c),
+                                P("pcn", c, c + 1), EQ, MUL), e_oh)
+            inc(V.tensor_scalar(cols(T.oh, c, 128), T.i128[:], P("tqf", c, c + 1), None, EQ), e_oh)
+        wait(PE, e_oh)
+        for c in range(2):
+            m = PE.matmul(T.pd[:, 0:32], cols(T.oh, c, 128), P("mv", 32 * c, 32 * c + 32), c == 0, c == 1)
+        e_pd = one(m)
+        if o:
+            wait(PE, C["idn"])
+            for c in range(2):
+                m = PE.matmul(T.ph1[:, 128 * c:128 * c + 128], cols(T.oh, c, 128), T.idn[:], True, True)
+            e_tr = one(m)
         wait(V, e_pgt, e_gw0)
         e_gw = one(V.tensor_copy(T.gw[0:16, :], T.pp[0:16, 0:16]))
+        wait(V, e_pd)
+        R["g"] = one(V.tensor_copy(own_table, T.pd[:, 0:32]))
+        if o == 1:
+            wait(V, rem("gin", NL), R["g"])
+            R["gm"] = one(V.tensor_tensor(T.gms[:], T.gme[:], T.gt[:, 0:32], MAX))
+        if o:
+            wait(S, e_tr)
+            R["t1"] = one(S.activation(T.t1[:], T.ph1[:, 0:CAPP], COPY))
+            R["m2"] = one(V.tensor_scalar(P("m2"), P("mv"), 0.0, None, GT))
         wait(V, e_gw, C["mk"])
         e_gd = one(V.tensor_tensor(T.gd[:], T.gw[:].indirect(T.rep[:, 0:16]), T.mk[:], MUL))
         wait(PE, e_gd, e_onf)
         e_pg = one(PE.matmul(T.pg[:, 0:CAPP], T.onf[:, 0:128], T.gd[:], True, True))
         wait(S, e_pg)
         R["gr"] = one(S.activation(T.gr[:], T.pg[:, 0:CAPP], COPY))
-        R["ow"] = e_ow
         return R
 
     def largest(n, *es):
@@ -285,77 +297,63 @@ def rank_program(g, core, T, topo):
         if o > 1:
             inc(V.memset(T.gt[:, 0:32], 0.0), e_gt0)
         consts_first()
-        consts_rest()
+        consts_neg()
+        consts_mid()
         if i in RAW_RELAY:
             wait(g, rem("rlin", NL))
             fused(xfer(T.rlx[:], T.raw[:], [serves(home, q) for q in RAW_RELAY[i]], "rawin", off_chip))
-        if i < 4:
-            h2, late = SECOND[i]
-            h2 = hs[h2]
-            ds = [serves(home, q) for q in range(1, N) if q not in late]
+        consts_rest()
+        wait(PE, C["mk"])
+        e = one(PE.matmul(T.po[:, 0:128], T.mk[0:16, 0:128], T.mk[0:16, 0:128], True, True))
+        wait(S, e)
+        e_lmt = one(S.activation(T.lmt[:], T.po[:, 0:128], COPY))
+        if i in RELAY:
+            f = RELAY.index(i)
             wait(g, rem("rin", 4))
-            fused(xfer(T.rel[:], cols(T.wk, i, 128), ds, "wA" if i < 2 else "wB", off_chip),
-                  xfer(T.rel[:], T.rel2[:] if i == 3 else T.rel[:], [h2], "rin", chip_bits(h2)))
+            fused(xfer(T.rel[:], cols(T.wk, f, 128), [serves(home, q) for q in range(1, N)],
+                       "wA" if f < 2 else "wB", off_chip))
 
         e_raw = rem("rawin", len(off_chip))
         R = make_lists(e_raw, [e_raw], T.gme[:])
         lb = chip_bits(rcore)
         wait(g, R["off"])
         fused(xfer(T.off[:], cols(T.lin, o, 16), [rcore], "l%d" % o, lb))
-        if i == 6:
-            d2, d3 = [[serves(home, q) for q in SECOND[f][1]] for f in (2, 3)]
-            n = len(off_chip) // 2
-            wait(g, rem("rin", 2 * NL))
-            fused(xfer(T.rel[:], cols(T.wk, 2, 128), d2, "wB", off_chip[:n]),
-                  xfer(T.rel2[:], cols(T.wk, 3, 128), d3, "wB", off_chip[n:]))
-        elif i >= 4:
-            wait(g, rem("rin", NL))
-            fused(xfer(T.rel[:], cols(T.wk, i - 4, 128), [serves(home, q) for q in SECOND[i - 4][1]], "wA", off_chip))
-        if o > 1:
-            wait(g, R["g"])
-            fused(xfer(T.gme[:], cols(T.gt, o, 32), hs[o:] + [rcore], "gin", lb))
+        table = T.gms if o == 1 else T.gme
+        wait(g, R["gm"] if o == 1 else R["g"])
+        fused(xfer(table[:], cols(T.gt, o, 32), hs[o:] + [rcore], "gin", lb))
 
-        e_dsl = one(V.tensor_scalar(P("dsl"), T.pd[:, 0:32], 1.0, None, SUB))
-        wait(V, e_dsl)
-        e = ev()
-        inc(V.tensor_scalar(P("dsi", 0, 32), P("dsl"), 15, None, AND), e)
-        inc(V.tensor_scalar(P("dsi", 32, 64), P("dsl"), 4, None, SHR), e)
-        wait(V, e)
-        e_rqs = one(V.tensor_tensor(T.rqs[:], P("dsi", 32, 64).indirect(T.rep[:]), T.i16[:], EQ))
-        e_lhs = one(V.tensor_tensor(T.lhs[:], P("dsi", 0, 32).indirect(T.rep[:]), T.i16[:], EQ))
-        e_gin = rem("gin", NL * max(1, o - 1))
-        if o == 1:
-            wait(V, e_gin, R["g"])
-            e = one(V.tensor_tensor(T.gms[:], T.gme[:], T.gt[:, 0:32], MAX))
-            wait(g, e)
-            fused(xfer(T.gms[:], cols(T.gt, o, 32), hs[o:] + [rcore], "gin", lb))
-        win, es = largest(o, e_gin, e_gt0)
-        wait(V, e_rqs, *es)
-        e_rps = one(V.tensor_tensor(T.rps[:], win.indirect(T.rep[:]), T.rqs[:], MUL))
-        wait(PE, e_lhs, e_rps, R["ow"])
-        for c in range(32):
-            m = PE.matmul(T.pl[0:16, 0:16], cols(T.lhs, c, 16), cols(T.rps, c, 16), c == 0, c == 31)
+        win, es = largest(o, rem("gin", NL * max(1, o - 1)), e_gt0)
+        wait(PE, R["t1"], R["g"], *es)
+        for c in range(2):
+            m = PE.matmul(T.pd[:, 32 * c:32 * c + 32], cols(T.t1, c, 128), win, True, True)
         e = one(m)
+        wait(V, e, R["m2"])
+        e = one(V.tensor_tensor(P("prd"), T.pd[:, 0:64], P("m2"), MUL))
         wait(V, e)
-        e_pw = one(V.tensor_copy(T.pw[0:16, :], T.pl[0:16, 0:16]))
+        e = ev()
+        for c in range(2):
+            inc(V.tensor_reduce(P("pv", c, c + 1), P("prd", 32 * c, 32 * c + 32), AX, ADD), e)
+        wait(V, e)
+        e_rr = ev()
+        for c in range(2):
+            inc(V.tensor_scalar(P("rr", 8 * c, 8 * c + 8), P("m16", 8 * c, 8 * c + 8), P("pv", c, c + 1), None, MUL), e_rr)
 
         w = T.wk
-        n_wb = sum(len(off_chip) // (2 if o in SECOND[f][1] else 1) for f in (2, 3))
         b = bits(rcore)
-        wait(PE, rem("wA", 2 * len(off_chip)), rem("xin", len(b) if o == 7 else len(b) // 2))
+        wait(PE, rem("wA", 2 * len(off_chip)), rem("xin", len(b) // max(len(grp) for grp in GROUPS if o in grp)))
         e_a = one(PE.matmul(T.ph0[:, 0:CAPP], cols(w, 0, 128), T.xk[:], True, True))
-        wait(PE, e_pw, R["off"])
-        e = one(PE.matmul(T.pc[:, 0:16], T.mk[0:16, 0:128], T.pw[0:16, :], True, True))
         e_b = one(PE.matmul(T.ph1[:, 0:CAPP], cols(w, 1, 128), T.xk[:], True, True))
-        wait(V, e)
-        e_prv = one(V.tensor_copy(T.prv[:], T.pc[:, 0:16]))
-        wait(g, e_prv)
-        fused(xfer(T.prv[:], cols(T.pin, o, 16), [rcore], "p%d" % o, lb))
+        wait(PE, e_rr, e_lmt, R["off"])
+        e_pv = one(PE.matmul(T.pc[:, 0:16], T.lmt[:], P("rr"), True, True))
         wait(S, e_a)
         e_h0 = one(S.activation(T.h0[:], T.ph0[:, 0:CAPP], RELU))
         wait(V, e_b)
         e_h1 = one(V.tensor_scalar(T.h1[:], T.ph1[:, 0:CAPP], 0.0, None, MAX))
-        wait(PE, rem("wB", n_wb), e_h0)
+        wait(V, e_pv)
+        e_prv = one(V.tensor_copy(T.prv[:], T.pc[:, 0:16]))
+        wait(g, e_prv)
+        fused(xfer(T.prv[:], cols(T.pin, o, 16), [rcore], "p%d" % o, lb))
+        wait(PE, rem("wB", 2 * len(off_chip)), e_h0)
         PE.matmul(T.po[:, 0:CAPP], cols(w, 2, 128), T.h0[:], True, False)
         wait(PE, e_h1)
         e_o = one(PE.matmul(T.po[:, 0:CAPP], cols(w, 3, 128), T.h1[:], False, True))
@@ -377,14 +375,16 @@ def rank_program(g, core, T, topo):
         wait(g, e_pf, e_gt)
         fused(xfer(T.raw[:], T.raw[:], [serves(home, q) for q in DIRECT], "rawin", off_chip),
               xfer(T.raw[:], T.rlx[:], [hs[h] for h in RAW_RELAY], "rlin", chip_bits(hs[0])))
+        consts_neg()
         wait(g, e_w1, e_w2)
         b = bits(hs[0])
         order = chip_bits(hs[0]) + off_chip
-        fused(*[xfer(cols(T.wr, f, 128), T.rel[:], [hs[f]], "rin", order[4 * f:4 * f + 4]) for f in range(4)])
+        fused(*[xfer(cols(T.wr, f, 128), T.rel[:], [hs[RELAY[f]]], "rin", order[4 * f:4 * f + 4]) for f in range(4)])
         g.sem_inc(T.sem.go, 1)
         wait(SY, rem("go", 1))
         e_x1 = one(SY.dma_start(T.xw[:, X0:TOK], T.x[:, X0:TOK]), 16)
 
+        consts_mid()
         consts_rest()
         R = make_lists(e_pf, [e_gt], T.gt[:, 0:32])
         e_pci = one(g.iota(P("pci"), [[0, 1]], 0, 1))
@@ -399,7 +399,7 @@ def rank_program(g, core, T, topo):
         el = {q: rem("l%d" % q, NL) for q in range(1, N)}
         wait(V, e_x0, e_x1)
         wait(S, e_x0, e_x1)
-        for grp in ((1, 2), (3, 4), (5, 6), (7,)):
+        for grp in GROUPS:
             es = []
             for q in grp:
                 dst, src = cols(T.tx, q, CAPP), T.xw[:].indirect(lists[q])
@@ -423,6 +423,10 @@ def rank_program(g, core, T, topo):
         e_h0 = one(S.activation(T.h0[:], T.ph0[:, 0:CAPP], RELU))
         wait(S, e_b)
         e_h1 = one(S.activation(T.h1[:], T.ph1[:, 0:CAPP], RELU))
+        wait(PE, e_h0)
+        PE.matmul(T.po[:, 0:CAPP], cols(T.wr, 2, 128), T.h0[:], True, False)
+        wait(PE, e_h1)
+        e_o = one(PE.matmul(T.po[:, 0:CAPP], cols(T.wr, 3, 128), T.h1[:], False, True))
 
         wait(V, e_pci)
         e = ev()
@@ -432,22 +436,17 @@ def rank_program(g, core, T, topo):
         e = one(V.tensor_copy(P("pcf"), P("pcb")))
         wait(V, e, e_rci, C["i16"])
         e_rpc = one(V.tensor_scalar(T.repc[:], P("rci"), P("pcf", 0, 1), None, ADD))
-        e_rlm = one(V.tensor_scalar(T.rlm[:], T.i16[:, 0:128], P("pcf", 1, 2), None, EQ))
+        e_rlm = one(V.tensor_scalar(T.rlm[:], T.i16[:], P("pcf", 1, 2), None, EQ))
         win, es = largest(N, rem("gin", NL * 7), R["g"])
         wait(V, e_rpc, e_ki, *es)
         e_ix = one(V.tensor_tensor(T.ivx[:], win.indirect(T.repc[:]), T.mki[:], MUL))
         wait(PE, e_ix, e_rlm, R["ow"])
         e = one(PE.matmul(T.pl[:, 0:CAPP], T.rlm[:], T.ivx[:], True, True))
+        wait(V, e_o, R["gr"])
+        acc = [e_z, one(V.tensor_tensor(T.acc[:, Z:Z + CAPP], T.po[:, 0:CAPP], T.gr[:], MUL))]
         wait(V, e)
         e_inv = one(V.tensor_copy(T.inv[:], T.pl[:, 0:CAPP]))
 
-        wait(PE, e_h0)
-        PE.matmul(T.po[:, 0:CAPP], cols(T.wr, 2, 128), T.h0[:], True, False)
-        wait(PE, e_h1)
-        e_o = one(PE.matmul(T.po[:, 0:CAPP], cols(T.wr, 3, 128), T.h1[:], False, True))
-
-        wait(V, e_o, R["gr"])
-        acc = [e_z, one(V.tensor_tensor(T.acc[:, Z:Z + CAPP], T.po[:, 0:CAPP], T.gr[:], MUL))]
         for q in range(1, N):
             wait(V, rem("p%d" % q, NL), rem("r%d" % q, len(b)), *acc)
             lim = Z + CAPP * q

from concourse.bass import DstId, RemoteDMATransfer
from concourse.mybir import AluOpType, ActivationFunctionType, AxisListType

N, TOK, CAPP = 8, 4096, 256
SIM_CORES = 256
Z = 16
X0 = 512
BIG = 1024.0
PIECES = (256, 640, 1024, 1280, 896)

F, I, B, U = "float32", "int32", "bfloat16", "uint16"


def sb(n, dtype):
    return ("sbuf", [128, n], dtype)


SMALL = {}


def pack(buf, items):
    a = 0
    for name, n in items:
        SMALL[name] = (buf, a, n)
        a += (n + 7) // 8 * 8
    return a


N_INT = pack("ints", [("rpi", 32), ("gi", 8), ("gsi", 16), ("tsi", 2), ("tqi", 4), ("pci", 1), ("pcb", 2), ("rci", 16)])
N_FLT = pack("flts", [("mm", 16), ("tk1", 8), ("pcf", 2), ("m0", 16), ("m16", 16), ("pcn", 2), ("pcm", 16), ("tsf", 2),
                      ("tqf", 4), ("mv", 64), ("m2", 64), ("prd", 64), ("pv", 2), ("rr", 16),
                      ("mx1", 128), ("mx2", 64), ("mx3", 32), ("lh", 128), ("rq", 128), ("rv", 128), ("rg", 128)])

SCRATCH = {
    "ints": sb(N_INT, I), "flts": sb(N_FLT, F),
    "pk": sb(8, I), "wr": sb(512, F), "xw": sb(TOK, F), "yw": sb(TOK, F),
    "acc": sb(Z + N * CAPP, F), "res": sb(N * CAPP, F), "tx": sb(N * CAPP, F),
    "lin": sb(N * 16, U), "pin": sb(N * 16, U), "repc": sb(16, U),
    "mk0": sb(CAPP, F), "mki": sb(CAPP, F), "rlm": sb(128, F), "ivx": sb(CAPP, F), "inv": sb(CAPP, U),
    "rel": sb(128, F), "rlx": sb(16, F),
    "wk": sb(512, F), "xk": sb(CAPP, F), "rk": sb(CAPP, F), "gme": sb(32, F), "gms": sb(32, F),
    "prv": sb(16, U), "idn": sb(128, F), "lmt": sb(128, F), "t1": sb(CAPP, F),
    "raw": sb(16, F),
    "onb": sb(128, B), "neb": sb(128, B), "ne0": sb(128, B), "neg": sb(128, B), "onf": sb(CAPP, F),
    "rep": sb(32, U), "i16": sb(128, F), "i128": sb(128, F), "mk": sb(CAPP, F),
    "m8": sb(8, B), "s8": sb(8, B),
    "ow": sb(16, F), "off": sb(16, U), "gw": sb(16, F), "gd": sb(CAPP, F), "gr": sb(CAPP, F),
    "oh": sb(CAPP, F), "gt": sb(N * 32, F),
    "h0": sb(CAPP, F), "h1": sb(CAPP, F),
}
for _n in ("pp", "pl", "pc", "pd", "pg", "ph0", "ph1", "po"):
    SCRATCH[_n] = ("psum", [128, 512], "float32")
NEV = 120
SEMAPHORES = (["sent", "rin", "rlin", "rawin", "wA", "wB", "xin", "gin", "go"]
              + [c + "%d" % o for c in "lpr" for o in range(1, N)] + ["e%d" % i for i in range(NEV)])

ADD, SUB, MUL, MAX = AluOpType.add, AluOpType.subtract, AluOpType.mult, AluOpType.max
EQ, NE, GE, GT = AluOpType.is_equal, AluOpType.not_equal, AluOpType.is_ge, AluOpType.is_gt
SHR, AND = AluOpType.arith_shift_right, AluOpType.bitwise_and
RELU, COPY = ActivationFunctionType.Relu, ActivationFunctionType.Copy
AX = AxisListType.X

RELAY = (0, 4, 2, 6)
DIRECT = (1, 2, 3, 4, 5)
RAW_RELAY = {3: (6,), 5: (7,)}
GROUPS = ((1,), (2,), (3, 4), (5, 6), (7,))


def chip_helpers(topo, rcore):
    cs = [c for c in range(SIM_CORES)
          if c != rcore and topo.host(c) == topo.host(rcore) and topo.chip(c) == topo.chip(rcore)]
    return [c for c in cs if topo.die(c) != topo.die(rcore)] + [c for c in cs if topo.die(c) == topo.die(rcore)]


def rank_program(g, core, T, topo):
    V, S, PE, SY = g.vector, g.scalar, g.tensor, g.sync
    cores = T.cores
    rank = T.rank_of(core)
    home = None
    for r in range(N):
        if topo.host(cores[r]) == topo.host(core) and topo.chip(cores[r]) == topo.chip(core):
            home = r
    if home is None:
        return
    helpers = {r: chip_helpers(topo, cores[r]) for r in range(N)}
    hs = helpers[home]
    o = 0 if rank is not None else hs.index(core) + 1
    cnt = [0]
    sent = [0]
    events = []
    done = {}

    def ev():
        e = [T.sem["e%d" % cnt[0]], 0, "e%d" % cnt[0], False]
        cnt[0] += 1
        events.append(e)
        return e

    def rem(name, n):
        e = [T.sem[name], n, name, False]
        events.append(e)
        return e

    def inc(ins, e, n=1):
        ins.then_inc(e[0], n)
        e[1] += n
        return e

    def one(ins, n=1):
        return inc(ins, ev(), n)

    def wait(q, *es):
        qn = "v" if q is V else "s" if q is S else "p" if q is PE else "y" if q is SY else "g"
        for e in es:
            if done.get((qn, e[2])) != e[1]:
                q.wait_ge(e[0], e[1])
                done[(qn, e[2])] = e[1]
                e[3] = True

    def P(name, a=0, b=None):
        buf, first, n = SMALL[name]
        return T[buf][:, first + a:first + (n if b is None else b)]

    def bits(dst):
        m = topo.mask(core, dst)
        return [b for b in range(16) if (m >> b) & 1]

    off_chip = bits(cores[(home + 1) % N])

    def chip_bits(dst):
        return [b for b in bits(dst) if b not in off_chip]

    NL = len(chip_bits(hs[o] if o == 0 else cores[home]))

    def did(dst):
        rid, pid = topo.addr(dst, core)
        return DstId(rid=rid, pnc=pid)

    def xfer(src, dst, dests, sem, bs):
        return RemoteDMATransfer(srcs=[src], dsts=[dst] * len(dests), dst_ids=[did(d) for d in dests],
                                 dma_engine_mask=sum(1 << b for b in bs), remote_sem=T.sem[sem]), len(bs)

    def fused(*trs):
        g.remote_dma_fused([t for t, _ in trs], local_sem=T.sem.sent)
        sent[0] += sum(n for _, n in trs)

    def cols(t, c, w):
        return t[:, c * w:(c + 1) * w]

    def serves(k, q):
        return helpers[(k - q) % N][q - 1]

    small = {"allow_small_or_imprecise_dtypes": True}
    C = {}

    def consts_first():
        C["rpi"] = one(g.iota(P("rpi"), [[1, 32]], 0, 0))
        wait(g, e_neb)
        C["ne0"] = one(g.affine_select(T.ne0[:], T.neb[:], [[-1, 128]], GT, 0.0, 0, 1))
        wait(V, C["rpi"])
        C["rep"] = one(V.tensor_copy(T.rep[:], P("rpi")))

    def consts_neg():
        wait(g, C["ne0"])
        C["neg"] = one(g.affine_select(T.neg[:], T.ne0[:], [[-1, 128]], NE, BIG, 0, 1))

    def consts_mid():
        C["i16"] = one(g.iota(T.i16[:], [[0, 8], [1, 16]], 0, 0, **small))
        wait(g, e_onf)
        C["m0"] = one(g.affine_select(P("m0"), T.onf[:, 0:16], [[0, 2], [-16, 8]], GE, 0.0, 0, 1))
        C["mk"] = one(g.affine_select(T.mk[:], T.onf[:], [[0, 16], [1, 16]], EQ, 0.0, 0, -1))

    def consts_rest():
        wait(g, C["m0"])
        C["m16"] = one(g.affine_select(P("m16"), P("m0"), [[0, 2], [16, 8]], GE, 0.0, 15, -1))
        C["i128"] = one(g.iota(T.i128[:], [[1, 128]], 0, 0, **small))
        C["pcn"] = one(g.iota(P("pcn"), [[128, 2]], Z + CAPP * o, 1, **small))
        if o:
            C["idn"] = one(g.affine_select(T.idn[:], T.onf[:, 0:128], [[-1, 128]], EQ, 0.0, 0, 1))

    e_neb = one(V.memset(T.neb[:], -1.0))
    e_onb = one(V.memset(T.onb[:], 1.0))
    e_onf = one(V.memset(T.onf[:], 1.0))
    e_gw0 = one(V.memset(T.gw[:], 0.0))

    def make_lists(e_pick, e_gate, own_table):
        R = {}
        pick, gate = T.raw[:, 0:8], T.raw[:, 8:16]
        rp8 = T.rep[:, 0:8]
        wait(V, e_pick)
        e = ev()
        inc(V.tensor_scalar(P("mm", 0, 8), pick, float(TOK * home), None, GE), e)
        inc(V.tensor_scalar(P("mm", 8, 16), pick, float(TOK * (home + 1)), None, GE), e)
        wait(V, e)
        e_m = one(V.tensor_tensor(T.m8[:], P("mm", 0, 8), P("mm", 8, 16), SUB))
        e_tk = one(V.tensor_scalar(P("tk1"), pick, float(1 - TOK * home), None, ADD))
        wait(V, e_m, e_onb)
        e_s = one(V.tensor_tensor_scan(T.s8[:], T.onb[:, 0:8], T.m8[:], 0.0, MUL, ADD))
        wait(PE, e_s, e_m, e_onb, C["neg"])
        PE.matmul(T.pp[:, 0:8], T.onb[:], T.s8[:], True, False)
        e_p = one(PE.matmul(T.pp[:, 0:8], T.neg[:], T.m8[:], False, True))
        wait(V, e_p)
        e_gi = one(V.tensor_scalar(P("gi"), T.pp[:, 0:8], BIG + 1.0, None, SUB))
        wait(V, e_gi)
        e_gsi = ev()
        inc(V.tensor_scalar(P("gsi", 8, 16), P("gi"), 4, None, SHR), e_gsi)
        inc(V.tensor_scalar(P("gsi", 0, 8), P("gi"), 15, None, AND), e_gsi)
        wait(V, e_gsi, C["rep"], C["i16"])
        e_rq = one(V.tensor_tensor(P("rq"), P("gsi", 8, 16).indirect(rp8), T.i16[:], EQ))
        e_lh = one(V.tensor_tensor(P("lh"), P("gsi", 0, 8).indirect(rp8), T.i16[:], EQ))
        wait(V, e_rq, e_tk)
        e_rv = one(V.tensor_tensor(P("rv"), P("tk1").indirect(rp8), P("rq"), MUL))
        wait(PE, e_lh, e_rv)
        for c in range(8):
            m = PE.matmul(T.pl[0:16, 0:16], P("lh", 16 * c, 16 * c + 16), P("rv", 16 * c, 16 * c + 16), c == 0, c == 7)
        e_pl = one(m)
        wait(V, *e_gate)
        e_rg = one(V.tensor_tensor(P("rg"), gate.indirect(rp8), P("rq"), MUL))
        wait(V, e_pl)
        R["ow"] = one(V.tensor_copy(T.ow[0:16, :], T.pl[0:16, 0:16]))
        wait(PE, R["ow"], C["mk"])
        e_pc = one(PE.matmul(T.pc[:, 0:16], T.mk[0:16, 0:128], T.ow[0:16, :], True, True))
        wait(PE, e_rg, e_gi)
        for c in range(8):
            m = PE.matmul(T.pp[0:16, 0:16], P("lh", 16 * c, 16 * c + 16), P("rg", 16 * c, 16 * c + 16), c == 0, c == 7)
        e_pgt = one(m)
        wait(V, e_pc)
        R["off"] = one(V.tensor_scalar(T.off[:], T.pc[:, 0:16], 1.0, None, SUB))
        wait(V, C["m16"])
        e = one(V.tensor_tensor(P("pcm"), T.pc[:, 0:16], P("m16"), MUL))
        wait(V, e)
        e = ev()
        for c in range(2):
            inc(V.tensor_reduce(P("tsf", c, c + 1), P("pcm", 8 * c, 8 * c + 8), AX, ADD), e)
        wait(V, e)
        e = one(V.tensor_scalar(P("tsi"), P("tsf"), 1.0, None, SUB))
        wait(V, e)
        e = ev()
        inc(V.tensor_scalar(P("tqi", 0, 2), P("tsi"), 127, None, AND), e)
        inc(V.tensor_scalar(P("tqi", 2, 4), P("tsi"), 7, None, SHR), e)
        wait(V, e)
        e = one(V.tensor_copy(P("tqf"), P("tqi")))
        wait(V, e, C["i128"], C["pcn"])
        e_oh = ev()
        for c in range(2):
            inc(V.tensor_scalar(P("mv", 32 * c, 32 * c + 32), T.i128[:, 0:32], P("tqf", 2 + c, 3 + c),
                                P("pcn", c, c + 1), EQ, MUL), e_oh)
            inc(V.tensor_scalar(cols(T.oh, c, 128), T.i128[:], P("tqf", c, c + 1), None, EQ), e_oh)
        wait(PE, e_oh)
        for c in range(2):
            m = PE.matmul(T.pd[:, 0:32], cols(T.oh, c, 128), P("mv", 32 * c, 32 * c + 32), c == 0, c == 1)
        e_pd = one(m)
        if o:
            wait(PE, C["idn"])
            for c in range(2):
                m = PE.matmul(T.ph1[:, 128 * c:128 * c + 128], cols(T.oh, c, 128), T.idn[:], True, True)
            e_tr = one(m)
        wait(V, e_pgt, e_gw0)
        e_gw = one(V.tensor_copy(T.gw[0:16, :], T.pp[0:16, 0:16]))
        wait(V, e_pd)
        R["g"] = one(V.tensor_copy(own_table, T.pd[:, 0:32]))
        if o == 1:
            wait(V, rem("gin", NL), R["g"])
            R["gm"] = one(V.tensor_tensor(T.gms[:], T.gme[:], T.gt[:, 0:32], MAX))
        if o:
            wait(S, e_tr)
            R["t1"] = one(S.activation(T.t1[:], T.ph1[:, 0:CAPP], COPY))
            R["m2"] = one(V.tensor_scalar(P("m2"), P("mv"), 0.0, None, GT))
        wait(V, e_gw, C["mk"])
        e_gd = one(V.tensor_tensor(T.gd[:], T.gw[:].indirect(T.rep[:, 0:16]), T.mk[:], MUL))
        wait(PE, e_gd, e_onf)
        e_pg = one(PE.matmul(T.pg[:, 0:CAPP], T.onf[:, 0:128], T.gd[:], True, True))
        wait(S, e_pg)
        R["gr"] = one(S.activation(T.gr[:], T.pg[:, 0:CAPP], COPY))
        return R

    def largest(n, *es):
        wait(V, *es)
        if n == 1:
            return T.gt[:, 0:32], es
        if n == 2:
            return T.gt[:, 32:64], es
        if n <= 4:
            e = one(V.tensor_tensor(P("mx2"), T.gt[:, 0:64], T.gt[:, 64:128], MAX))
        else:
            e = one(V.tensor_tensor(P("mx1"), T.gt[:, 0:128], T.gt[:, 128:256], MAX))
            wait(V, e)
            e = one(V.tensor_tensor(P("mx2"), P("mx1", 0, 64), P("mx1", 64, 128), MAX))
        wait(V, e)
        e = one(V.tensor_tensor(P("mx3"), P("mx2", 0, 32), P("mx2", 32, 64), MAX))
        return P("mx3"), (e,)

    if rank is None:
        rcore = cores[home]
        i = o - 1
        e_gt0 = one(V.memset(T.gt[:, 32 * o:N * 32], 0.0))
        if o > 1:
            inc(V.memset(T.gt[:, 0:32], 0.0), e_gt0)
        consts_first()
        consts_neg()
        consts_mid()
        if i in RAW_RELAY:
            wait(g, rem("rlin", NL))
            fused(xfer(T.rlx[:], T.raw[:], [serves(home, q) for q in RAW_RELAY[i]], "rawin", off_chip))
        consts_rest()
        wait(PE, C["mk"])
        e = one(PE.matmul(T.po[:, 0:128], T.mk[0:16, 0:128], T.mk[0:16, 0:128], True, True))
        wait(S, e)
        e_lmt = one(S.activation(T.lmt[:], T.po[:, 0:128], COPY))
        if i in RELAY:
            f = RELAY.index(i)
            wait(g, rem("rin", 4))
            fused(xfer(T.rel[:], cols(T.wk, f, 128), [serves(home, q) for q in range(1, N)],
                       "wA" if f < 2 else "wB", off_chip))

        e_raw = rem("rawin", len(off_chip))
        R = make_lists(e_raw, [e_raw], T.gme[:])
        lb = chip_bits(rcore)
        wait(g, R["off"])
        fused(xfer(T.off[:], cols(T.lin, o, 16), [rcore], "l%d" % o, lb))
        table = T.gms if o == 1 else T.gme
        wait(g, R["gm"] if o == 1 else R["g"])
        fused(xfer(table[:], cols(T.gt, o, 32), hs[o:] + [rcore], "gin", lb))

        win, es = largest(o, rem("gin", NL * max(1, o - 1)), e_gt0)
        wait(PE, R["t1"], R["g"], *es)
        for c in range(2):
            m = PE.matmul(T.pd[:, 32 * c:32 * c + 32], cols(T.t1, c, 128), win, True, True)
        e = one(m)
        wait(V, e, R["m2"])
        e = one(V.tensor_tensor(P("prd"), T.pd[:, 0:64], P("m2"), MUL))
        wait(V, e)
        e = ev()
        for c in range(2):
            inc(V.tensor_reduce(P("pv", c, c + 1), P("prd", 32 * c, 32 * c + 32), AX, ADD), e)
        wait(V, e)
        e_rr = ev()
        for c in range(2):
            inc(V.tensor_scalar(P("rr", 8 * c, 8 * c + 8), P("m16", 8 * c, 8 * c + 8), P("pv", c, c + 1), None, MUL), e_rr)

        w = T.wk
        b = bits(rcore)
        wait(PE, rem("wA", 2 * len(off_chip)), rem("xin", len(b) // max(len(grp) for grp in GROUPS if o in grp)))
        e_a = one(PE.matmul(T.ph0[:, 0:CAPP], cols(w, 0, 128), T.xk[:], True, True))
        e_b = one(PE.matmul(T.ph1[:, 0:CAPP], cols(w, 1, 128), T.xk[:], True, True))
        wait(PE, e_rr, e_lmt, R["off"])
        e_pv = one(PE.matmul(T.pc[:, 0:16], T.lmt[:], P("rr"), True, True))
        wait(S, e_a)
        e_h0 = one(S.activation(T.h0[:], T.ph0[:, 0:CAPP], RELU))
        wait(V, e_b)
        e_h1 = one(V.tensor_scalar(T.h1[:], T.ph1[:, 0:CAPP], 0.0, None, MAX))
        wait(V, e_pv)
        e_prv = one(V.tensor_copy(T.prv[:], T.pc[:, 0:16]))
        wait(g, e_prv)
        fused(xfer(T.prv[:], cols(T.pin, o, 16), [rcore], "p%d" % o, lb))
        wait(PE, rem("wB", 2 * len(off_chip)), e_h0)
        PE.matmul(T.po[:, 0:CAPP], cols(w, 2, 128), T.h0[:], True, False)
        wait(PE, e_h1)
        e_o = one(PE.matmul(T.po[:, 0:CAPP], cols(w, 3, 128), T.h1[:], False, True))
        wait(V, e_o, R["gr"])
        e_r = one(V.tensor_tensor(T.rk[:], T.po[:, 0:CAPP], T.gr[:], MUL))
        wait(g, e_r)
        fused(xfer(T.rk[:], cols(T.res, o, CAPP), [rcore], "r%d" % o, b))
    else:
        e_pk = one(SY.dma_start(T.pk[:], T.pick[:]), 16)
        e_gt = one(S.dma_start(T.raw[:, 8:16], T.gate[:]), 16)
        e_w1 = one(SY.dma_start(T.wr[:, 0:256], T.w1[:]), 16)
        e_w2 = one(S.dma_start(T.wr[:, 256:512], T.w2[:]), 16)
        e_x0 = one(SY.dma_start(T.xw[:, 0:X0], T.x[:, 0:X0]), 16)
        e_z = one(V.memset(T.acc[:, 0:Z], 0.0))
        consts_first()
        wait(V, e_pk)
        e_pf = one(V.tensor_copy(T.raw[:, 0:8], T.pk[:]))

        wait(g, e_pf, e_gt)
        fused(xfer(T.raw[:], T.raw[:], [serves(home, q) for q in DIRECT], "rawin", off_chip),
              xfer(T.raw[:], T.rlx[:], [hs[h] for h in RAW_RELAY], "rlin", chip_bits(hs[0])))
        consts_neg()
        wait(g, e_w1, e_w2)
        b = bits(hs[0])
        order = chip_bits(hs[0]) + off_chip
        fused(*[xfer(cols(T.wr, f, 128), T.rel[:], [hs[RELAY[f]]], "rin", order[4 * f:4 * f + 4]) for f in range(4)])
        g.sem_inc(T.sem.go, 1)
        wait(SY, rem("go", 1))
        e_x1 = one(SY.dma_start(T.xw[:, X0:TOK], T.x[:, X0:TOK]), 16)

        consts_mid()
        consts_rest()
        R = make_lists(e_pf, [e_gt], T.gt[:, 0:32])
        e_pci = one(g.iota(P("pci"), [[0, 1]], 0, 1))
        e_rci = one(g.iota(P("rci"), [[2, 16]], 0, 0))
        wait(g, R["g"])
        fused(xfer(T.gt[:, 0:32], T.gt[:, 0:32], [hs[0]], "gin", chip_bits(hs[0])))
        e_k0 = one(g.affine_select(T.mk0[:], T.onf[:], [[0, 32], [-16, 8]], GE, 0.0, 0, 1))
        wait(g, e_k0)
        e_ki = one(g.affine_select(T.mki[:], T.mk0[:], [[0, 32], [16, 8]], GE, 0.0, 15, -1))

        lists = {q: cols(T.lin, q, 16) for q in range(1, N)}
        el = {q: rem("l%d" % q, NL) for q in range(1, N)}
        wait(V, e_x0, e_x1)
        wait(S, e_x0, e_x1)
        for grp in GROUPS:
            es = []
            for q in grp:
                dst, src = cols(T.tx, q, CAPP), T.xw[:].indirect(lists[q])
                if q % 2:
                    wait(V, el[q])
                    es.append(one(V.tensor_copy(dst, src)))
                else:
                    wait(S, el[q])
                    es.append(one(S.activation(dst, src, COPY)))
            wait(g, *es)
            n = len(b) // len(grp)
            fused(*[xfer(cols(T.tx, q, CAPP), T.xk[:], [hs[q - 1]], "xin", bits(hs[q - 1])[n * j:n * j + n])
                    for j, q in enumerate(grp)])

        wait(S, R["off"])
        e_t0 = one(S.activation(T.tx[:, 0:CAPP], T.xw[:].indirect(T.off[:]), COPY))
        wait(PE, e_t0, e_w1, e_w2)
        e_a = one(PE.matmul(T.ph0[:, 0:CAPP], cols(T.wr, 0, 128), T.tx[:, 0:CAPP], True, True))
        e_b = one(PE.matmul(T.ph1[:, 0:CAPP], cols(T.wr, 1, 128), T.tx[:, 0:CAPP], True, True))
        wait(S, e_a)
        e_h0 = one(S.activation(T.h0[:], T.ph0[:, 0:CAPP], RELU))
        wait(S, e_b)
        e_h1 = one(S.activation(T.h1[:], T.ph1[:, 0:CAPP], RELU))
        wait(PE, e_h0)
        PE.matmul(T.po[:, 0:CAPP], cols(T.wr, 2, 128), T.h0[:], True, False)
        wait(PE, e_h1)
        e_o = one(PE.matmul(T.po[:, 0:CAPP], cols(T.wr, 3, 128), T.h1[:], False, True))

        wait(V, e_pci)
        e = ev()
        inc(V.tensor_scalar(P("pcb", 0, 1), P("pci"), 15, 3, AND, SHR), e)
        inc(V.tensor_scalar(P("pcb", 1, 2), P("pci"), 15, None, AND), e)
        wait(V, e)
        e = one(V.tensor_copy(P("pcf"), P("pcb")))
        wait(V, e, e_rci, C["i16"])
        e_rpc = one(V.tensor_scalar(T.repc[:], P("rci"), P("pcf", 0, 1), None, ADD))
        e_rlm = one(V.tensor_scalar(T.rlm[:], T.i16[:], P("pcf", 1, 2), None, EQ))
        win, es = largest(N, rem("gin", NL * 7), R["g"])
        wait(V, e_rpc, e_ki, *es)
        e_ix = one(V.tensor_tensor(T.ivx[:], win.indirect(T.repc[:]), T.mki[:], MUL))
        wait(PE, e_ix, e_rlm, R["ow"])
        e = one(PE.matmul(T.pl[:, 0:CAPP], T.rlm[:], T.ivx[:], True, True))
        wait(V, e_o, R["gr"])
        acc = [e_z, one(V.tensor_tensor(T.acc[:, Z:Z + CAPP], T.po[:, 0:CAPP], T.gr[:], MUL))]
        wait(V, e)
        e_inv = one(V.tensor_copy(T.inv[:], T.pl[:, 0:CAPP]))

        for q in range(1, N):
            wait(V, rem("p%d" % q, NL), rem("r%d" % q, len(b)), *acc)
            lim = Z + CAPP * q
            acc.append(one(V.tensor_tensor(T.acc[:, lim:lim + CAPP], T.acc[:, 0:lim].indirect(cols(T.pin, q, 16)),
                                           cols(T.res, q, CAPP), ADD)))
        wait(V, e_inv, *acc)
        wait(S, e_inv, *acc)
        es, a = [], 0
        for n in PIECES:
            h = a + n // 2
            e1 = one(V.tensor_copy(T.yw[:, a:h], T.acc[:].indirect(T.inv[:, a // 16:h // 16])))
            e2 = one(S.activation(T.yw[:, h:a + n], T.acc[:].indirect(T.inv[:, h // 16:(a + n) // 16]), COPY))
            wait(SY, e1, e2)
            es.append(one(SY.dma_start(T.y[:, a:a + n], T.yw[:, a:a + n]), 16))
            a += n
        wait(SY, *es)

    for e in events:
        if not e[3]:
            wait(g, e)
    g.wait_ge(T.sem.sent, sent[0])
